import numpy as np
import ml_dtypes


def mxq(x, axis, fmt="e4m3"):
    dtype, down = {"e4m3": (ml_dtypes.float8_e4m3fn, 7), "e5m2": (ml_dtypes.float8_e5m2, 14)}[fmt]
    v = np.moveaxis(np.asarray(x, np.float32).astype(ml_dtypes.bfloat16).astype(np.float64), axis, -1)
    blocks = v.reshape(v.shape[:-1] + (-1, 32))
    amax = np.abs(blocks).max(-1, keepdims=True)
    byte = np.maximum(np.where(amax > 0, np.frexp(amax)[1] - 1 + 127, 0) - down, 1)
    scale = np.exp2(byte - 127.0)
    codes = (blocks / scale).astype(np.float32).astype(dtype).astype(np.float64)
    return np.moveaxis((codes * scale).reshape(v.shape), -1, axis)


WIDE = False


def mx_kscale(k):
    if not WIDE:
        return np.ones(k)
    levels = np.array([10, -10, 5, -5, 0])
    if k % 512:
        return np.exp2(np.random.permutation(np.resize(levels, k // 32))).repeat(32)
    a = np.empty((k // 512, 16))
    for p in range(k // 512):
        a[p, :8] = np.random.permutation(np.resize(levels, 8))
        for g in range(8):
            far = levels[np.abs(levels - a[p, g]) >= 10]
            a[p, g + 8] = far[np.random.randint(len(far))]
    return np.exp2(a.ravel()).repeat(32)


def f64(x):
    return np.asarray(x).astype(np.float64)


def striped(idx):
    return np.tile(idx.reshape(-1, 16).T, (8, 1)).astype(np.uint16)


def unstriped(offs):
    return offs[:16].T.reshape(-1).astype(np.int64)


def striped8(idx):
    return np.concatenate([x.reshape(-1, 16).T for x in idx]).astype(np.uint16)


def runs(offs, k):
    lists = np.stack([offs[16 * r : 16 * r + 16].T.reshape(-1) for r in range(8)]).astype(np.int64)
    return lists[np.arange(k) % 512 // 64]


def pack_weight(w):
    k, n = w.shape
    w = f64(np.asarray(w, np.float32).astype(ml_dtypes.bfloat16)).reshape(k // 32, 32, n)
    amax = np.abs(w).max(1)
    byte = np.clip(np.where(amax > 0, np.frexp(amax)[1] - 1 + 127 - 7, 1), 1, 254)
    scaled = (w * np.exp2(127.0 - byte)[:, None, :]).reshape(k, n).astype(np.float32)
    words = np.ascontiguousarray(scaled.reshape(k // 512, 128, 4, n).transpose(0, 1, 3, 2)).astype(ml_dtypes.float8_e4m3fn).view(np.uint8)
    return words, np.ascontiguousarray(byte.astype(np.uint8).reshape(k // 512, 16, n))


def unpack_weight(words, scales):
    g, p, n, _ = words.shape
    vals = np.ascontiguousarray(words).view(ml_dtypes.float8_e4m3fn).astype(np.float64) * np.repeat(np.exp2(scales.astype(np.float64) - 127.0), 8, axis=1)[..., None]
    return vals.transpose(0, 1, 3, 2).reshape(g * 512, n)


def sigmoid(v):
    return 1.0 / (1.0 + np.exp(-np.maximum(v, -700.0)))


K, T, S, N, G, H = 512, 2048, 512, 512, 2048, 512


def setup_inputs():
    n = np.random.standard_normal
    s = mx_kscale(K)[:, None]
    u = mx_kscale(H)
    packed_xT = pack_weight(n((K, T)) * s)
    packed_dT = pack_weight(n((K, G)) / s)
    return {
        "x_words": packed_xT[0],
        "x_scales": packed_xT[1],
        "d_words": packed_dT[0],
        "d_scales": packed_dT[1],
        "gn": (np.random.uniform(0.5, 1.5, (H, 1)) * u[:, None]).astype(np.float32),
        "w1": (n((H, N)) / np.sqrt(H) / u[:, None]).astype(np.float32),
        "w2": (n((K, N)) / np.sqrt(K) / s).astype(np.float32),
        "offs": striped(np.random.permutation(T)[:S]),
        "kidx": striped8(np.random.randint(0, G, (8, H))),
        "own": striped(np.random.permutation(T)[:S]),
    }


def reference(x_words, x_scales, d_words, d_scales, gn, w1, w2, offs, kidx, own):
    d_kidx = unpack_weight(d_words, d_scales)[np.arange(K)[:, None], runs(kidx, K)]
    xq = unpack_weight(x_words, x_scales)[:, unstriped(offs)]
    s = sigmoid(0.0625 * (d_kidx.T @ xq))
    z = f64(gn) * s
    h = mxq(f64(w1), 0, "e4m3").T @ mxq(z, 0, "e4m3")
    x_own = unpack_weight(x_words, x_scales)[:, unstriped(own)]
    val = mxq(f64(w2), 0, "e4m3").T @ x_own
    return h * val

@@ -1,0 +1,214 @@
+from contextlib import ExitStack
+
+import concourse.mybir as mybir
+
+K, T, S, N, G, H = 512, 2048, 512, 512, 2048, 512
+FLOPS = 2 * K * H * S + 2 * H * N * S + 2 * K * N * S
+
+F32 = mybir.dt.float32
+BF16 = mybir.dt.bfloat16
+I32 = mybir.dt.int32
+U32 = mybir.dt.uint32
+U16 = mybir.dt.uint16
+U8 = mybir.dt.uint8
+FP8X4 = mybir.dt.float8_e4m3fn_x4
+SIGMOID = mybir.ActivationFunctionType.Sigmoid
+MULT = mybir.AluOpType.mult
+
+P = 128
+PACK = 4
+HALF = S // 2
+CHUNK = 128
+
+
+def tile_picked_twostage_sigmoid_p_kernel(
+    tc, x_words, x_scales, d_words, d_scales, gn, w1, w2, offs, kidx, own, out
+):
+    nc = tc.nc
+    with ExitStack() as ctx:
+        keep = ctx.enter_context(tc.tile_pool(name="keep", bufs=1))
+        psum = ctx.enter_context(tc.psum_pool(name="psum", bufs=4))
+
+        def sb(name, width, dtype, slot=None):
+            return keep.tile([P, width], dtype, name=name, tag=slot or name, align_bytes=64)
+
+        kidx_t = keep.tile([P, H // 16], U16, name="kidx_t")
+        offs_t = keep.tile([P, S // 16], U16, name="offs_t")
+        own_t = keep.tile([P, S // 16], U16, name="own_t")
+
+        d_scale_win = sb("d_scale_win", G, U8)
+        x_scale_win = sb("x_scale_win", T, U8)
+        d_plane = sb("d_plane", H, U8)
+        warm = sb("warm", 16, F32)
+        nc.vector.memset(x_scale_win[:].bitcast(I32), 0)
+        nc.vector.memset(d_plane[:].bitcast(I32), 0)
+        nc.vector.memset(warm[:, 0:1], 0.0)
+
+        w_raw = sb("w_raw", PACK * N, F32)
+        d_win = sb("d_win", G, I32)
+        gn_t = sb("gn_t", PACK, F32)
+
+        nc.sync.dma_start(kidx_t[:], kidx)
+        nc.sync.dma_start(
+            d_scale_win[:].bitcast(I32),
+            d_scales[0].bitcast(I32).unsqueeze(1).to_broadcast([16, 8, G // 4]),
+        )
+        nc.sync.dma_start(offs_t[:], offs)
+        nc.sync.dma_start(d_win[:], d_words[0].rearrange("p c r -> p (c r)").bitcast(I32))
+        nc.sync.dma_start(own_t[:], own)
+        for q in range(4):
+            nc.sync.dma_start(
+                x_scale_win[32 * q : 32 * q + 4, :].bitcast(I32),
+                x_scales[0, 4 * q : 4 * q + 4, :].bitcast(I32),
+            )
+        nc.sync.dma_start(w_raw[:], w2.rearrange("(p j) n -> p (j n)", j=PACK))
+        nc.sync.dma_start(gn_t[:], gn.rearrange("(p t) o -> p (t o)", t=PACK))
+        x_win = sb("x_win", T, I32)
+        nc.sync.dma_start(x_win[:], x_words[0].rearrange("p c r -> p (c r)").bitcast(I32))
+        nc.scalar.activation(warm[:, 8:9], warm[:, 0:1], SIGMOID)
+
+        d_scale_g = sb("d_scale_g", H, U8)
+        nc.vector.tensor_copy(d_scale_g[:], d_scale_win[:].indirect(kidx_t[:]))
+        d_scale_p = sb("d_scale_p", H, U8)
+        nc.vector.tensor_copy(
+            d_scale_p[:].rearrange("p (t m) -> p m t", t=PACK),
+            d_scale_g[:].rearrange("p (m t) -> p m t", t=PACK),
+        )
+        for r in range(4):
+            nc.sync.dma_start(
+                d_plane[r:P:32, :].bitcast(I32),
+                d_scale_p[8 * r : P : 32, :].bitcast(I32),
+            )
+        w1_raw = sb("w1_raw", PACK * N, F32, "d_scale_g")
+        nc.sync.dma_start(w1_raw[:], w1.rearrange("(p j) n -> p (j n)", j=PACK))
+
+        d_g = sb("d_g", H, U32)
+        nc.vector.tensor_copy(d_g[:], d_win[:].bitcast(U32).indirect(kidx_t[:]))
+        xq_plane = sb("xq_plane", S, U8)
+        nc.vector.tensor_copy(xq_plane[:], x_scale_win[:].indirect(offs_t[:]))
+        d_p = sb("d_p", H, U32)
+        nc.vector.tensor_copy(
+            d_p[:].rearrange("p (t m) -> p m t", t=PACK),
+            d_g[:].rearrange("p (m t) -> p m t", t=PACK),
+        )
+        xo_plane = sb("xo_plane", S, U8)
+        nc.vector.tensor_copy(xo_plane[:], x_scale_win[:].indirect(own_t[:]))
+
+        w2_b = sb("w2_b", PACK * N, BF16)
+        nc.scalar.copy(
+            w2_b[:].rearrange("p (n j) -> p n j", j=PACK),
+            w_raw[:].rearrange("p (j n) -> p n j", j=PACK),
+        )
+
+        xq = []
+        for a in range(2):
+            t_ = sb(f"xq{a}", HALF, U32, ("x_scale_win", "xq1")[a])
+            nc.vector.tensor_copy(
+                t_[:], x_win[:].bitcast(U32).indirect(offs_t[:, a * 16 : (a + 1) * 16])
+            )
+            xq.append(t_)
+        xo = sb("xo", S, U32)
+        nc.vector.tensor_copy(xo[:], x_win[:].bitcast(U32).indirect(own_t[:]))
+        w2_q = sb("w2_q", N, U32, "x_win")
+        w2_s = sb("w2_s", N, U8)
+        nc.vector.quantize_mx(w2_q[:].bitcast(FP8X4), w2_s[:], w2_b[:])
+
+        sig = []
+        for c in range(S // CHUNK):
+            bank = psum.tile([P, PACK * CHUNK], F32, name=f"score{c}", tag="chain")
+            cols = slice((c % 2) * CHUNK, (c % 2 + 1) * CHUNK)
+            for t in range(PACK):
+                nc.tensor.matmul_mx(
+                    out=bank[:, t * CHUNK : (t + 1) * CHUNK],
+                    lhsT=d_p[:, t * P : (t + 1) * P].bitcast(FP8X4),
+                    lhsT_scale=d_plane[:, t * P : (t + 1) * P],
+                    rhs=xq[c // 2][:, cols].bitcast(FP8X4),
+                    rhs_scale=xq_plane[:, c * CHUNK : (c + 1) * CHUNK],
+                    start=True,
+                    stop=True,
+                )
+            s_ = sb(f"sig{c}", PACK * CHUNK, F32)
+            nc.scalar.activation(
+                s_[:].rearrange("p (j t) -> p j t", t=PACK),
+                bank[:].rearrange("p (t j) -> p j t", t=PACK),
+                SIGMOID,
+                scale=0.0625,
+            )
+            sig.append(s_)
+
+        val_bank = []
+        for m in range(N // P):
+            bank = psum.tile([P, S], F32, name=f"valb{m}", tag="chain")
+            nc.tensor.matmul_mx(
+                out=bank[:],
+                lhsT=w2_q[:, m * P : (m + 1) * P].bitcast(FP8X4),
+                lhsT_scale=w2_s[:, m * P : (m + 1) * P],
+                rhs=xo[:].bitcast(FP8X4),
+                rhs_scale=xo_plane[:],
+                start=True,
+                stop=True,
+            )
+            val_bank.append(bank)
+
+        gn_b = gn_t[:].unsqueeze(1).to_broadcast([P, CHUNK, PACK])
+        z_q = sb("z_q", S, U32)
+        z_s = sb("z_s", S, U8)
+        z_b = [sb(f"z_b{a}", PACK * HALF, BF16) for a in range(2)]
+
+        def weigh(c):
+            o = (c % 2) * PACK * CHUNK
+            nc.vector.tensor_tensor(
+                z_b[c // 2][:, o : o + PACK * CHUNK].rearrange("p (j t) -> p j t", t=PACK),
+                sig[c][:].rearrange("p (j t) -> p j t", t=PACK),
+                gn_b,
+                MULT,
+            )
+
+        def quant_z(a):
+            cols = slice(a * HALF, (a + 1) * HALF)
+            nc.vector.quantize_mx(z_q[:, cols].bitcast(FP8X4), z_s[:, cols], z_b[a][:])
+
+        w1_b = [sb(f"w1_b{a}", PACK * 256, BF16, ("xq1", None)[a]) for a in range(2)]
+        w1_q = [sb(f"w1_q{a}", 256, U32) for a in range(2)]
+        w1_s = [sb(f"w1_s{a}", 256, U8) for a in range(2)]
+        val = [sb(f"val{m}", S, F32) for m in range(N // P)]
+        res = [sb(f"res{m}", S, F32) for m in range(N // P)]
+
+        def weave_w1(a):
+            nc.scalar.copy(
+                w1_b[a][:].rearrange("p (n j) -> p n j", j=PACK),
+                w1_raw[:].rearrange("p (j n) -> p n j", j=PACK)[:, a * 256 : (a + 1) * 256, :],
+            )
+
+        def quant_w1(a):
+            nc.vector.quantize_mx(w1_q[a][:].bitcast(FP8X4), w1_s[a][:], w1_b[a][:])
+
+        def finish(m):
+            bank = psum.tile([P, S], F32, name=f"h{m}", tag="h")
+            cols = slice((m % 2) * P, (m % 2 + 1) * P)
+            nc.tensor.matmul_mx(
+                out=bank[:],
+                lhsT=w1_q[m // 2][:, cols].bitcast(FP8X4),
+                lhsT_scale=w1_s[m // 2][:, cols],
+                rhs=z_q[:].bitcast(FP8X4),
+                rhs_scale=z_s[:],
+                start=True,
+                stop=True,
+            )
+            nc.vector.tensor_tensor(res[m][:], bank[:], val[m][:], MULT)
+            nc.sync.dma_start(out[m * P : (m + 1) * P, :], res[m][:])
+
+        weigh(0)
+        weigh(1)
+        weigh(2)
+        quant_z(0)
+        weigh(3)
+        weave_w1(0)
+        weave_w1(1)
+        quant_w1(0)
+        quant_z(1)
+        quant_w1(1)
+        for m in range(N // P):
+            nc.scalar.copy(val[m][:], val_bank[m][:])
+        for m in range(N // P):
+            finish(m)

@@ -40,6 +40,7 @@ def tile_picked_twostage_sigmoid_p_kernel(
         x_scale_win = sb("x_scale_win", T, U8)
         d_plane = sb("d_plane", H, U8)
         warm = sb("warm", 16, F32)
+        nc.vector.memset(d_scale_win[:].bitcast(I32), 0)
         nc.vector.memset(x_scale_win[:].bitcast(I32), 0)
         nc.vector.memset(d_plane[:].bitcast(I32), 0)
         nc.vector.memset(warm[:, 0:1], 0.0)
@@ -49,20 +50,17 @@ def tile_picked_twostage_sigmoid_p_kernel(
         gn_t = sb("gn_t", PACK, F32)
 
         nc.sync.dma_start(kidx_t[:], kidx)
-        nc.sync.dma_start(
-            d_scale_win[:].bitcast(I32),
-            d_scales[0].bitcast(I32).unsqueeze(1).to_broadcast([16, 8, G // 4]),
-        )
         nc.sync.dma_start(offs_t[:], offs)
-        nc.sync.dma_start(d_win[:], d_words[0].rearrange("p c r -> p (c r)").bitcast(I32))
         nc.sync.dma_start(own_t[:], own)
+        nc.sync.dma_start(gn_t[:], gn.rearrange("(p t) o -> p (t o)", t=PACK))
+        nc.sync.dma_start(d_scale_win[0:P:8, :].bitcast(I32), d_scales[0].bitcast(I32))
+        nc.sync.dma_start(d_win[:], d_words[0].rearrange("p c r -> p (c r)").bitcast(I32))
         for q in range(4):
             nc.sync.dma_start(
                 x_scale_win[32 * q : 32 * q + 4, :].bitcast(I32),
                 x_scales[0, 4 * q : 4 * q + 4, :].bitcast(I32),
             )
         nc.sync.dma_start(w_raw[:], w2.rearrange("(p j) n -> p (j n)", j=PACK))
-        nc.sync.dma_start(gn_t[:], gn.rearrange("(p t) o -> p (t o)", t=PACK))
         x_win = sb("x_win", T, I32)
         nc.sync.dma_start(x_win[:], x_words[0].rearrange("p c r -> p (c r)").bitcast(I32))
         nc.scalar.activation(warm[:, 8:9], warm[:, 0:1], SIGMOID)
@@ -95,10 +93,9 @@ def tile_picked_twostage_sigmoid_p_kernel(
         nc.vector.tensor_copy(xo_plane[:], x_scale_win[:].indirect(own_t[:]))
 
         w2_b = sb("w2_b", PACK * N, BF16)
-        nc.scalar.copy(
-            w2_b[:].rearrange("p (n j) -> p n j", j=PACK),
-            w_raw[:].rearrange("p (j n) -> p n j", j=PACK),
-        )
+        w2_dst = w2_b[:].rearrange("p (c i j) -> p c j i", i=4, j=PACK)
+        w2_src = w_raw[:].rearrange("p (j c i) -> p c j i", i=4, j=PACK)
+        nc.scalar.copy(w2_dst, w2_src)
 
         xq = []
         for a in range(2):
@@ -176,8 +173,8 @@ def tile_picked_twostage_sigmoid_p_kernel(
 
         def weave_w1(a):
             nc.scalar.copy(
-                w1_b[a][:].rearrange("p (n j) -> p n j", j=PACK),
-                w1_raw[:].rearrange("p (j n) -> p n j", j=PACK)[:, a * 256 : (a + 1) * 256, :],
+                w1_b[a][:].rearrange("p (c i j) -> p c j i", i=4, j=PACK),
+                w1_raw[:].rearrange("p (j c i) -> p c j i", i=4, j=PACK)[:, a * 64 : (a + 1) * 64],
             )
 
         def quant_w1(a):

@@ -14,6 +14,7 @@ U8 = mybir.dt.uint8
 FP8X4 = mybir.dt.float8_e4m3fn_x4
 SIGMOID = mybir.ActivationFunctionType.Sigmoid
 MULT = mybir.AluOpType.mult
+ADD = mybir.AluOpType.add
 
 P = 128
 PACK = 4
@@ -39,76 +40,75 @@ def tile_picked_twostage_sigmoid_p_kernel(
         d_scale_win = sb("d_scale_win", G, U8)
         x_scale_win = sb("x_scale_win", T, U8)
         d_plane = sb("d_plane", H, U8)
-        warm = sb("warm", 16, F32)
         nc.vector.memset(d_scale_win[:].bitcast(I32), 0)
         nc.vector.memset(x_scale_win[:].bitcast(I32), 0)
         nc.vector.memset(d_plane[:].bitcast(I32), 0)
-        nc.vector.memset(warm[:, 0:1], 0.0)
 
-        w_raw = sb("w_raw", PACK * N, F32)
         d_win = sb("d_win", G, I32)
+        x_win = sb("x_win", T, I32)
         gn_t = sb("gn_t", PACK, F32)
 
         nc.sync.dma_start(kidx_t[:], kidx)
         nc.sync.dma_start(offs_t[:], offs)
-        nc.sync.dma_start(own_t[:], own)
-        nc.sync.dma_start(gn_t[:], gn.rearrange("(p t) o -> p (t o)", t=PACK))
         nc.sync.dma_start(d_scale_win[0:P:8, :].bitcast(I32), d_scales[0].bitcast(I32))
-        nc.sync.dma_start(d_win[:], d_words[0].rearrange("p c r -> p (c r)").bitcast(I32))
         for q in range(4):
             nc.sync.dma_start(
                 x_scale_win[32 * q : 32 * q + 4, :].bitcast(I32),
                 x_scales[0, 4 * q : 4 * q + 4, :].bitcast(I32),
             )
-        nc.sync.dma_start(w_raw[:], w2.rearrange("(p j) n -> p (j n)", j=PACK))
-        x_win = sb("x_win", T, I32)
+        nc.sync.dma_start(d_win[:], d_words[0].rearrange("p c r -> p (c r)").bitcast(I32))
+        nc.sync.dma_start(own_t[:], own)
         nc.sync.dma_start(x_win[:], x_words[0].rearrange("p c r -> p (c r)").bitcast(I32))
-        nc.scalar.activation(warm[:, 8:9], warm[:, 0:1], SIGMOID)
+        nc.sync.dma_start(gn_t[:], gn.rearrange("(p t) o -> p (t o)", t=PACK))
 
         d_scale_g = sb("d_scale_g", H, U8)
         nc.vector.tensor_copy(d_scale_g[:], d_scale_win[:].indirect(kidx_t[:]))
         d_scale_p = sb("d_scale_p", H, U8)
         nc.vector.tensor_copy(
-            d_scale_p[:].rearrange("p (t m) -> p m t", t=PACK),
-            d_scale_g[:].rearrange("p (m t) -> p m t", t=PACK),
+            d_scale_p[:].rearrange("p (t m) -> p t m", t=PACK),
+            d_scale_g[:].rearrange("p (m t) -> p t m", t=PACK),
         )
         for r in range(4):
             nc.sync.dma_start(
                 d_plane[r:P:32, :].bitcast(I32),
                 d_scale_p[8 * r : P : 32, :].bitcast(I32),
             )
-        w1_raw = sb("w1_raw", PACK * N, F32, "d_scale_g")
-        nc.sync.dma_start(w1_raw[:], w1.rearrange("(p j) n -> p (j n)", j=PACK))
 
-        d_g = sb("d_g", H, U32)
-        nc.vector.tensor_copy(d_g[:], d_win[:].bitcast(U32).indirect(kidx_t[:]))
+        def load_w(w, raw, a):
+            nc.sync.dma_start(
+                raw[a].rearrange("p (j n) -> p j n", j=PACK),
+                w.rearrange("(p j) n -> p j n", j=PACK)[:, :, a * 256 : (a + 1) * 256],
+            )
+
+        w_raw = sb("w_raw", 4 * PACK * 256, F32, "d_scale_g")
+        w2_raw = [w_raw[:, a * 1024 : (a + 1) * 1024] for a in range(2)]
+        w1_raw = [w_raw[:, a * 1024 : (a + 1) * 1024] for a in range(2, 4)]
+        load_w(w2, w2_raw, 0)
+        load_w(w2, w2_raw, 1)
+        load_w(w1, w1_raw, 0)
+        load_w(w1, w1_raw, 1)
+
         xq_plane = sb("xq_plane", S, U8)
         nc.vector.tensor_copy(xq_plane[:], x_scale_win[:].indirect(offs_t[:]))
+        d_g = sb("d_g", H, U32)
+        nc.vector.tensor_copy(d_g[:], d_win[:].bitcast(U32).indirect(kidx_t[:]))
+        xo_plane = sb("xo_plane", S, U8)
+        nc.vector.tensor_copy(xo_plane[:], x_scale_win[:].indirect(own_t[:]))
         d_p = sb("d_p", H, U32)
         nc.vector.tensor_copy(
             d_p[:].rearrange("p (t m) -> p m t", t=PACK),
             d_g[:].rearrange("p (m t) -> p m t", t=PACK),
         )
-        xo_plane = sb("xo_plane", S, U8)
-        nc.vector.tensor_copy(xo_plane[:], x_scale_win[:].indirect(own_t[:]))
-
-        w2_b = sb("w2_b", PACK * N, BF16)
-        w2_dst = w2_b[:].rearrange("p (c i j) -> p c j i", i=4, j=PACK)
-        w2_src = w_raw[:].rearrange("p (j c i) -> p c j i", i=4, j=PACK)
-        nc.scalar.copy(w2_dst, w2_src)
 
         xq = []
         for a in range(2):
-            t_ = sb(f"xq{a}", HALF, U32, ("x_scale_win", "xq1")[a])
+            t_ = sb(f"xq{a}", HALF, U32)
             nc.vector.tensor_copy(
                 t_[:], x_win[:].bitcast(U32).indirect(offs_t[:, a * 16 : (a + 1) * 16])
             )
             xq.append(t_)
         xo = sb("xo", S, U32)
         nc.vector.tensor_copy(xo[:], x_win[:].bitcast(U32).indirect(own_t[:]))
-        w2_q = sb("w2_q", N, U32, "x_win")
-        w2_s = sb("w2_s", N, U8)
-        nc.vector.quantize_mx(w2_q[:].bitcast(FP8X4), w2_s[:], w2_b[:])
 
         sig = []
         for c in range(S // CHUNK):
@@ -133,20 +133,6 @@ def tile_picked_twostage_sigmoid_p_kernel(
             )
             sig.append(s_)
 
-        val_bank = []
-        for m in range(N // P):
-            bank = psum.tile([P, S], F32, name=f"valb{m}", tag="chain")
-            nc.tensor.matmul_mx(
-                out=bank[:],
-                lhsT=w2_q[:, m * P : (m + 1) * P].bitcast(FP8X4),
-                lhsT_scale=w2_s[:, m * P : (m + 1) * P],
-                rhs=xo[:].bitcast(FP8X4),
-                rhs_scale=xo_plane[:],
-                start=True,
-                stop=True,
-            )
-            val_bank.append(bank)
-
         gn_b = gn_t[:].unsqueeze(1).to_broadcast([P, CHUNK, PACK])
         z_q = sb("z_q", S, U32)
         z_s = sb("z_s", S, U8)
@@ -165,23 +151,40 @@ def tile_picked_twostage_sigmoid_p_kernel(
             cols = slice(a * HALF, (a + 1) * HALF)
             nc.vector.quantize_mx(z_q[:, cols].bitcast(FP8X4), z_s[:, cols], z_b[a][:])
 
-        w1_b = [sb(f"w1_b{a}", PACK * 256, BF16, ("xq1", None)[a]) for a in range(2)]
+        w2_b = [sb(f"w2_b{a}", PACK * 256, BF16, (None, "xq1")[a]) for a in range(2)]
+        w1_b = [sb(f"w1_b{a}", PACK * 256, BF16) for a in range(2)]
+        w2_q = [sb(f"w2_q{a}", 256, U32) for a in range(2)]
+        w2_s = [sb(f"w2_s{a}", 256, U8) for a in range(2)]
         w1_q = [sb(f"w1_q{a}", 256, U32) for a in range(2)]
         w1_s = [sb(f"w1_s{a}", 256, U8) for a in range(2)]
         val = [sb(f"val{m}", S, F32) for m in range(N // P)]
         res = [sb(f"res{m}", S, F32) for m in range(N // P)]
 
-        def weave_w1(a):
-            nc.scalar.copy(
-                w1_b[a][:].rearrange("p (c i j) -> p c j i", i=4, j=PACK),
-                w1_raw[:].rearrange("p (j c i) -> p c j i", i=4, j=PACK)[:, a * 64 : (a + 1) * 64],
+        def weave(copy, dst, raw):
+            copy(
+                dst[:].rearrange("p (c i j) -> p c j i", i=4, j=PACK),
+                raw.rearrange("p (j c i) -> p c j i", i=4, j=PACK),
             )
 
-        def quant_w1(a):
-            nc.vector.quantize_mx(w1_q[a][:].bitcast(FP8X4), w1_s[a][:], w1_b[a][:])
+        def quant(q, s, b):
+            nc.vector.quantize_mx(q[:].bitcast(FP8X4), s[:], b[:])
+
+        def project(m):
+            bank = psum.tile([P, S], F32, name=f"valb{m}", tag="val")
+            cols = slice((m % 2) * P, (m % 2 + 1) * P)
+            nc.tensor.matmul_mx(
+                out=bank[:],
+                lhsT=w2_q[m // 2][:, cols].bitcast(FP8X4),
+                lhsT_scale=w2_s[m // 2][:, cols],
+                rhs=xo[:].bitcast(FP8X4),
+                rhs_scale=xo_plane[:],
+                start=True,
+                stop=True,
+            )
+            nc.scalar.copy(val[m][:], bank[:])
 
         def finish(m):
-            bank = psum.tile([P, S], F32, name=f"h{m}", tag="h")
+            bank = psum.tile([P, S], F32, name=f"h{m}", tag="chain")
             cols = slice((m % 2) * P, (m % 2 + 1) * P)
             nc.tensor.matmul_mx(
                 out=bank[:],
@@ -195,17 +198,28 @@ def tile_picked_twostage_sigmoid_p_kernel(
             nc.vector.tensor_tensor(res[m][:], bank[:], val[m][:], MULT)
             nc.sync.dma_start(out[m * P : (m + 1) * P, :], res[m][:])
 
+        def weave_part(copy, dst, raw, lo, hi):
+            copy(
+                dst[:].rearrange("p (c i j) -> p c j i", i=4, j=PACK)[:, lo:hi],
+                raw.rearrange("p (j c i) -> p c j i", i=4, j=PACK)[:, lo:hi],
+            )
+
+        weave(nc.vector.tensor_copy, w2_b[0], w2_raw[0])
+        weave(nc.scalar.copy, w2_b[1], w2_raw[1])
+        weave(nc.scalar.copy, w1_b[0], w1_raw[0])
+        weave_part(nc.scalar.copy, w1_b[1], w1_raw[1], 0, 32)
         weigh(0)
+        quant(w2_q[0], w2_s[0], w2_b[0])
         weigh(1)
         weigh(2)
         quant_z(0)
+        quant(w2_q[1], w2_s[1], w2_b[1])
         weigh(3)
-        weave_w1(0)
-        weave_w1(1)
-        quant_w1(0)
+        weave_part(nc.vector.tensor_copy, w1_b[1], w1_raw[1], 32, 64)
+        quant(w1_q[0], w1_s[0], w1_b[0])
         quant_z(1)
-        quant_w1(1)
-        for m in range(N // P):
-            nc.scalar.copy(val[m][:], val_bank[m][:])
-        for m in range(N // P):
+        quant(w1_q[1], w1_s[1], w1_b[1])
+        for m in range(4):
+            project(m)
+        for m in range(4):
             finish(m)

@@ -28,10 +28,14 @@ def tile_picked_twostage_sigmoid_p_kernel(
     nc = tc.nc
     with ExitStack() as ctx:
         keep = ctx.enter_context(tc.tile_pool(name="keep", bufs=1))
+        placed = ctx.enter_context(tc.tile_pool(name="placed", bufs=1))
         psum = ctx.enter_context(tc.psum_pool(name="psum", bufs=4))
 
         def sb(name, width, dtype, slot=None):
             return keep.tile([P, width], dtype, name=name, tag=slot or name, align_bytes=64)
+
+        def at(name, width, dtype, offset):
+            return placed.tile([P, width], dtype, name=name, align_bytes=64, offset=offset)
 
         kidx_t = keep.tile([P, H // 16], U16, name="kidx_t")
         offs_t = keep.tile([P, S // 16], U16, name="offs_t")
@@ -44,6 +48,10 @@ def tile_picked_twostage_sigmoid_p_kernel(
         nc.vector.memset(x_scale_win[:].bitcast(I32), 0)
         nc.vector.memset(d_plane[:].bitcast(I32), 0)
 
+        warm = sb("warm", 16, F32)
+        nc.gpsimd.memset(warm[:, 0:1], 0.0)
+        nc.scalar.activation(warm[:, 8:9], warm[:, 0:1], SIGMOID)
+
         d_win = sb("d_win", G, I32)
         x_win = sb("x_win", T, I32)
         gn_t = sb("gn_t", PACK, F32)
@@ -51,17 +59,17 @@ def tile_picked_twostage_sigmoid_p_kernel(
         nc.sync.dma_start(kidx_t[:], kidx)
         nc.sync.dma_start(offs_t[:], offs)
         nc.sync.dma_start(d_scale_win[0:P:8, :].bitcast(I32), d_scales[0].bitcast(I32))
+        nc.sync.dma_start(d_win[:], d_words[0].rearrange("p c r -> p (c r)").bitcast(I32))
         for q in range(4):
             nc.sync.dma_start(
                 x_scale_win[32 * q : 32 * q + 4, :].bitcast(I32),
                 x_scales[0, 4 * q : 4 * q + 4, :].bitcast(I32),
             )
-        nc.sync.dma_start(d_win[:], d_words[0].rearrange("p c r -> p (c r)").bitcast(I32))
-        nc.sync.dma_start(own_t[:], own)
         nc.sync.dma_start(x_win[:], x_words[0].rearrange("p c r -> p (c r)").bitcast(I32))
+        nc.sync.dma_start(own_t[:], own)
         nc.sync.dma_start(gn_t[:], gn.rearrange("(p t) o -> p (t o)", t=PACK))
 
-        d_scale_g = sb("d_scale_g", H, U8)
+        d_scale_g = at("d_scale_g", H, U8, 10240 - 256)
         nc.vector.tensor_copy(d_scale_g[:], d_scale_win[:].indirect(kidx_t[:]))
         d_scale_p = sb("d_scale_p", H, U8)
         nc.vector.tensor_copy(
@@ -80,20 +88,19 @@ def tile_picked_twostage_sigmoid_p_kernel(
                 w.rearrange("(p j) n -> p j n", j=PACK)[:, :, a * 256 : (a + 1) * 256],
             )
 
-        w_raw = sb("w_raw", 4 * PACK * 256, F32, "d_scale_g")
-        w2_raw = [w_raw[:, a * 1024 : (a + 1) * 1024] for a in range(2)]
-        w1_raw = [w_raw[:, a * 1024 : (a + 1) * 1024] for a in range(2, 4)]
+        w_first = at("w_first", PACK * 256, F32, 6144)
+        w_rest = at("w_rest", 3 * PACK * 256, F32, 10240)
+        w2_raw = [w_first[:], w_rest[:, 0:1024]]
+        w1_raw = [w_rest[:, a * 1024 : (a + 1) * 1024] for a in range(1, 3)]
         load_w(w2, w2_raw, 0)
         load_w(w2, w2_raw, 1)
         load_w(w1, w1_raw, 0)
         load_w(w1, w1_raw, 1)
 
-        xq_plane = sb("xq_plane", S, U8)
-        nc.vector.tensor_copy(xq_plane[:], x_scale_win[:].indirect(offs_t[:]))
         d_g = sb("d_g", H, U32)
         nc.vector.tensor_copy(d_g[:], d_win[:].bitcast(U32).indirect(kidx_t[:]))
-        xo_plane = sb("xo_plane", S, U8)
-        nc.vector.tensor_copy(xo_plane[:], x_scale_win[:].indirect(own_t[:]))
+        xq_plane = sb("xq_plane", S, U8)
+        nc.vector.tensor_copy(xq_plane[:], x_scale_win[:].indirect(offs_t[:]))
         d_p = sb("d_p", H, U32)
         nc.vector.tensor_copy(
             d_p[:].rearrange("p (t m) -> p m t", t=PACK),
@@ -107,9 +114,22 @@ def tile_picked_twostage_sigmoid_p_kernel(
                 t_[:], x_win[:].bitcast(U32).indirect(offs_t[:, a * 16 : (a + 1) * 16])
             )
             xq.append(t_)
+        xo_plane = sb("xo_plane", S, U8)
+        nc.vector.tensor_copy(xo_plane[:], x_scale_win[:].indirect(own_t[:]))
         xo = sb("xo", S, U32)
         nc.vector.tensor_copy(xo[:], x_win[:].bitcast(U32).indirect(own_t[:]))
 
+        w2_b = [sb("w2_b0", PACK * 256, BF16), at("w2_b1", PACK * 256, BF16, 8192)]
+
+        def weave(copy, dst, raw):
+            copy(
+                dst[:].rearrange("p (c i j) -> p c j i", i=4, j=PACK),
+                raw.rearrange("p (j c i) -> p c j i", i=4, j=PACK),
+            )
+
+        weave(nc.scalar.copy, w2_b[0], w2_raw[0])
+
+        sig_all = at("sig_all", PACK * S, F32, 0)
         sig = []
         for c in range(S // CHUNK):
             bank = psum.tile([P, PACK * CHUNK], F32, name=f"score{c}", tag="chain")
@@ -124,9 +144,9 @@ def tile_picked_twostage_sigmoid_p_kernel(
                     start=True,
                     stop=True,
                 )
-            s_ = sb(f"sig{c}", PACK * CHUNK, F32)
+            s_ = sig_all[:, c * PACK * CHUNK : (c + 1) * PACK * CHUNK]
             nc.scalar.activation(
-                s_[:].rearrange("p (j t) -> p j t", t=PACK),
+                s_.rearrange("p (j t) -> p j t", t=PACK),
                 bank[:].rearrange("p (t j) -> p j t", t=PACK),
                 SIGMOID,
                 scale=0.0625,
@@ -134,37 +154,27 @@ def tile_picked_twostage_sigmoid_p_kernel(
             sig.append(s_)
 
         gn_b = gn_t[:].unsqueeze(1).to_broadcast([P, CHUNK, PACK])
-        z_q = sb("z_q", S, U32)
+        z_q = at("z_q", S, U32, 8192)
         z_s = sb("z_s", S, U8)
-        z_b = [sb(f"z_b{a}", PACK * HALF, BF16) for a in range(2)]
+        z_b = sb("z_b", PACK * S, BF16)
 
         def weigh(c):
-            o = (c % 2) * PACK * CHUNK
+            o = c * PACK * CHUNK
             nc.vector.tensor_tensor(
-                z_b[c // 2][:, o : o + PACK * CHUNK].rearrange("p (j t) -> p j t", t=PACK),
-                sig[c][:].rearrange("p (j t) -> p j t", t=PACK),
+                z_b[:, o : o + PACK * CHUNK].rearrange("p (j t) -> p j t", t=PACK),
+                sig[c].rearrange("p (j t) -> p j t", t=PACK),
                 gn_b,
                 MULT,
             )
 
-        def quant_z(a):
-            cols = slice(a * HALF, (a + 1) * HALF)
-            nc.vector.quantize_mx(z_q[:, cols].bitcast(FP8X4), z_s[:, cols], z_b[a][:])
-
-        w2_b = [sb(f"w2_b{a}", PACK * 256, BF16, (None, "xq1")[a]) for a in range(2)]
-        w1_b = [sb(f"w1_b{a}", PACK * 256, BF16) for a in range(2)]
+        w1_first = sb("w1_first", PACK * 256, BF16)
+        w1_third = sb("w1_third", PACK * P, BF16)
         w2_q = [sb(f"w2_q{a}", 256, U32) for a in range(2)]
         w2_s = [sb(f"w2_s{a}", 256, U8) for a in range(2)]
-        w1_q = [sb(f"w1_q{a}", 256, U32) for a in range(2)]
-        w1_s = [sb(f"w1_s{a}", 256, U8) for a in range(2)]
+        w1_q = sb("w1_q", N, U32)
+        w1_s = sb("w1_s", N, U8)
         val = [sb(f"val{m}", S, F32) for m in range(N // P)]
         res = [sb(f"res{m}", S, F32) for m in range(N // P)]
-
-        def weave(copy, dst, raw):
-            copy(
-                dst[:].rearrange("p (c i j) -> p c j i", i=4, j=PACK),
-                raw.rearrange("p (j c i) -> p c j i", i=4, j=PACK),
-            )
 
         def quant(q, s, b):
             nc.vector.quantize_mx(q[:].bitcast(FP8X4), s[:], b[:])
@@ -185,11 +195,11 @@ def tile_picked_twostage_sigmoid_p_kernel(
 
         def finish(m):
             bank = psum.tile([P, S], F32, name=f"h{m}", tag="chain")
-            cols = slice((m % 2) * P, (m % 2 + 1) * P)
+            cols = slice(m * P, (m + 1) * P)
             nc.tensor.matmul_mx(
                 out=bank[:],
-                lhsT=w1_q[m // 2][:, cols].bitcast(FP8X4),
-                lhsT_scale=w1_s[m // 2][:, cols],
+                lhsT=w1_q[:, cols].bitcast(FP8X4),
+                lhsT_scale=w1_s[:, cols],
                 rhs=z_q[:].bitcast(FP8X4),
                 rhs_scale=z_s[:],
                 start=True,
@@ -200,25 +210,28 @@ def tile_picked_twostage_sigmoid_p_kernel(
 
         def weave_part(copy, dst, raw, lo, hi):
             copy(
-                dst[:].rearrange("p (c i j) -> p c j i", i=4, j=PACK)[:, lo:hi],
+                dst[:].rearrange("p (c i j) -> p c j i", i=4, j=PACK),
                 raw.rearrange("p (j c i) -> p c j i", i=4, j=PACK)[:, lo:hi],
             )
 
-        weave(nc.vector.tensor_copy, w2_b[0], w2_raw[0])
+        def quant_w1(b, lo, hi):
+            nc.vector.quantize_mx(w1_q[:, lo:hi].bitcast(FP8X4), w1_s[:, lo:hi], b[:])
+
         weave(nc.scalar.copy, w2_b[1], w2_raw[1])
-        weave(nc.scalar.copy, w1_b[0], w1_raw[0])
-        weave_part(nc.scalar.copy, w1_b[1], w1_raw[1], 0, 32)
+        weave(nc.scalar.copy, w1_first, w1_raw[0])
+        weave_part(nc.scalar.copy, w1_third, w1_raw[1], 0, 32)
         weigh(0)
         quant(w2_q[0], w2_s[0], w2_b[0])
         weigh(1)
         weigh(2)
-        quant_z(0)
-        quant(w2_q[1], w2_s[1], w2_b[1])
         weigh(3)
-        weave_part(nc.vector.tensor_copy, w1_b[1], w1_raw[1], 32, 64)
-        quant(w1_q[0], w1_s[0], w1_b[0])
-        quant_z(1)
-        quant(w1_q[1], w1_s[1], w1_b[1])
+        quant(w2_q[1], w2_s[1], w2_b[1])
+        quant(z_q, z_s, z_b)
+        quant_w1(w1_first, 0, 256)
+        w1_last = sb("w1_last", PACK * P, BF16, "w1_first")
+        weave_part(nc.vector.tensor_copy, w1_last, w1_raw[1], 32, 64)
+        quant_w1(w1_third, 256, 384)
+        quant_w1(w1_last, 384, 512)
         for m in range(4):
             project(m)
         for m in range(4):

@@ -52,14 +52,16 @@ def tile_picked_twostage_sigmoid_p_kernel(
         nc.gpsimd.memset(warm[:, 0:1], 0.0)
         nc.scalar.activation(warm[:, 8:9], warm[:, 0:1], SIGMOID)
 
-        d_win = sb("d_win", G, I32)
+        d_win = at("d_win", G, I32, 10240)
         x_win = sb("x_win", T, I32)
         gn_t = sb("gn_t", PACK, F32)
 
         nc.sync.dma_start(kidx_t[:], kidx)
         nc.sync.dma_start(offs_t[:], offs)
+        d_rows = d_words[0].rearrange("p c r -> p (c r)").bitcast(I32)
+        nc.sync.dma_start(d_win[:, 0:512], d_rows[:, 0:512])
         nc.sync.dma_start(d_scale_win[0:P:8, :].bitcast(I32), d_scales[0].bitcast(I32))
-        nc.sync.dma_start(d_win[:], d_words[0].rearrange("p c r -> p (c r)").bitcast(I32))
+        nc.sync.dma_start(d_win[:, 512:G], d_rows[:, 512:G])
         for q in range(4):
             nc.sync.dma_start(
                 x_scale_win[32 * q : 32 * q + 4, :].bitcast(I32),
@@ -67,9 +69,16 @@ def tile_picked_twostage_sigmoid_p_kernel(
             )
         nc.sync.dma_start(x_win[:], x_words[0].rearrange("p c r -> p (c r)").bitcast(I32))
         nc.sync.dma_start(own_t[:], own)
-        nc.sync.dma_start(gn_t[:], gn.rearrange("(p t) o -> p (t o)", t=PACK))
+        def load_w(w, raw, a):
+            nc.sync.dma_start(
+                raw[a].rearrange("p (j n) -> p j n", j=PACK),
+                w.rearrange("(p j) n -> p j n", j=PACK)[:, :, a * 256 : (a + 1) * 256],
+            )
 
-        d_scale_g = at("d_scale_g", H, U8, 10240 - 256)
+        w_first = at("w_first", PACK * 256, F32, 6144)
+        load_w(w2, [w_first[:]], 0)
+
+        d_scale_g = sb("d_scale_g", H, U8)
         nc.vector.tensor_copy(d_scale_g[:], d_scale_win[:].indirect(kidx_t[:]))
         d_scale_p = sb("d_scale_p", H, U8)
         nc.vector.tensor_copy(
@@ -82,23 +91,17 @@ def tile_picked_twostage_sigmoid_p_kernel(
                 d_scale_p[8 * r : P : 32, :].bitcast(I32),
             )
 
-        def load_w(w, raw, a):
-            nc.sync.dma_start(
-                raw[a].rearrange("p (j n) -> p j n", j=PACK),
-                w.rearrange("(p j) n -> p j n", j=PACK)[:, :, a * 256 : (a + 1) * 256],
-            )
+        nc.sync.dma_start(gn_t[:], gn.rearrange("(p t) o -> p (t o)", t=PACK))
 
-        w_first = at("w_first", PACK * 256, F32, 6144)
+        d_g = sb("d_g", H, U32)
+        nc.vector.tensor_copy(d_g[:], d_win[:].bitcast(U32).indirect(kidx_t[:]))
         w_rest = at("w_rest", 3 * PACK * 256, F32, 10240)
         w2_raw = [w_first[:], w_rest[:, 0:1024]]
         w1_raw = [w_rest[:, a * 1024 : (a + 1) * 1024] for a in range(1, 3)]
-        load_w(w2, w2_raw, 0)
         load_w(w2, w2_raw, 1)
         load_w(w1, w1_raw, 0)
         load_w(w1, w1_raw, 1)
 
-        d_g = sb("d_g", H, U32)
-        nc.vector.tensor_copy(d_g[:], d_win[:].bitcast(U32).indirect(kidx_t[:]))
         xq_plane = sb("xq_plane", S, U8)
         nc.vector.tensor_copy(xq_plane[:], x_scale_win[:].indirect(offs_t[:]))
         d_p = sb("d_p", H, U32)
@@ -180,7 +183,7 @@ def tile_picked_twostage_sigmoid_p_kernel(
             nc.vector.quantize_mx(q[:].bitcast(FP8X4), s[:], b[:])
 
         def project(m):
-            bank = psum.tile([P, S], F32, name=f"valb{m}", tag="val")
+            bank = psum.tile([P, S], F32, name=f"valb{m}", tag="chain")
             cols = slice((m % 2) * P, (m % 2 + 1) * P)
             nc.tensor.matmul_mx(
                 out=bank[:],
@@ -194,7 +197,7 @@ def tile_picked_twostage_sigmoid_p_kernel(
             nc.scalar.copy(val[m][:], bank[:])
 
         def finish(m):
-            bank = psum.tile([P, S], F32, name=f"h{m}", tag="chain")
+            bank = psum.tile([P, S], F32, name=f"h{m}", tag="h")
             cols = slice(m * P, (m + 1) * P)
             nc.tensor.matmul_mx(
                 out=bank[:],

@@ -1,6 +1,7 @@
 from contextlib import ExitStack
 
 import concourse.mybir as mybir
+from concourse.masks import make_identity
 
 K, T, S, N, G, H = 512, 2048, 512, 512, 2048, 512
 FLOPS = 2 * K * H * S + 2 * H * N * S + 2 * K * N * S
@@ -20,6 +21,7 @@ P = 128
 PACK = 4
 HALF = S // 2
 CHUNK = 128
+BANK = 2048
 
 
 def tile_picked_twostage_sigmoid_p_kernel(
@@ -44,9 +46,12 @@ def tile_picked_twostage_sigmoid_p_kernel(
         d_scale_win = sb("d_scale_win", G, U8)
         x_scale_win = sb("x_scale_win", T, U8)
         d_plane = sb("d_plane", H, U8)
+        ident = sb("ident", P, F32)
         nc.vector.memset(d_scale_win[:].bitcast(I32), 0)
         nc.vector.memset(x_scale_win[:].bitcast(I32), 0)
         nc.vector.memset(d_plane[:].bitcast(I32), 0)
+        nc.vector.memset(ident[:], 0.0)
+        make_identity(nc, ident[:], nomemset=True)
 
         warm = sb("warm", 16, F32)
         nc.gpsimd.memset(warm[:, 0:1], 0.0)
@@ -57,11 +62,11 @@ def tile_picked_twostage_sigmoid_p_kernel(
         gn_t = sb("gn_t", PACK, F32)
 
         nc.sync.dma_start(kidx_t[:], kidx)
-        nc.sync.dma_start(offs_t[:], offs)
         d_rows = d_words[0].rearrange("p c r -> p (c r)").bitcast(I32)
         nc.sync.dma_start(d_win[:, 0:512], d_rows[:, 0:512])
         nc.sync.dma_start(d_scale_win[0:P:8, :].bitcast(I32), d_scales[0].bitcast(I32))
         nc.sync.dma_start(d_win[:, 512:G], d_rows[:, 512:G])
+        nc.sync.dma_start(offs_t[:], offs)
         for q in range(4):
             nc.sync.dma_start(
                 x_scale_win[32 * q : 32 * q + 4, :].bitcast(I32),
@@ -69,6 +74,7 @@ def tile_picked_twostage_sigmoid_p_kernel(
             )
         nc.sync.dma_start(x_win[:], x_words[0].rearrange("p c r -> p (c r)").bitcast(I32))
         nc.sync.dma_start(own_t[:], own)
+
         def load_w(w, raw, a):
             nc.sync.dma_start(
                 raw[a].rearrange("p (j n) -> p j n", j=PACK),
@@ -80,17 +86,11 @@ def tile_picked_twostage_sigmoid_p_kernel(
 
         d_scale_g = sb("d_scale_g", H, U8)
         nc.vector.tensor_copy(d_scale_g[:], d_scale_win[:].indirect(kidx_t[:]))
-        d_scale_p = sb("d_scale_p", H, U8)
-        nc.vector.tensor_copy(
-            d_scale_p[:].rearrange("p (t m) -> p t m", t=PACK),
-            d_scale_g[:].rearrange("p (m t) -> p t m", t=PACK),
-        )
         for r in range(4):
             nc.sync.dma_start(
                 d_plane[r:P:32, :].bitcast(I32),
-                d_scale_p[8 * r : P : 32, :].bitcast(I32),
+                d_scale_g[8 * r : P : 32, :].bitcast(I32),
             )
-
         nc.sync.dma_start(gn_t[:], gn.rearrange("(p t) o -> p (t o)", t=PACK))
 
         d_g = sb("d_g", H, U32)
@@ -104,12 +104,6 @@ def tile_picked_twostage_sigmoid_p_kernel(
 
         xq_plane = sb("xq_plane", S, U8)
         nc.vector.tensor_copy(xq_plane[:], x_scale_win[:].indirect(offs_t[:]))
-        d_p = sb("d_p", H, U32)
-        nc.vector.tensor_copy(
-            d_p[:].rearrange("p (t m) -> p m t", t=PACK),
-            d_g[:].rearrange("p (m t) -> p m t", t=PACK),
-        )
-
         xq = []
         for a in range(2):
             t_ = sb(f"xq{a}", HALF, U32)
@@ -122,7 +116,8 @@ def tile_picked_twostage_sigmoid_p_kernel(
         xo = sb("xo", S, U32)
         nc.vector.tensor_copy(xo[:], x_win[:].bitcast(U32).indirect(own_t[:]))
 
-        w2_b = [sb("w2_b0", PACK * 256, BF16), at("w2_b1", PACK * 256, BF16, 8192)]
+        w2_b = [sb("w2_b0", PACK * 256, BF16), sb("w2_b1", PACK * 256, BF16)]
+        w1_b = [sb("w1_b0", PACK * 256, BF16), sb("w1_b1", PACK * 256, BF16)]
 
         def weave(copy, dst, raw):
             copy(
@@ -130,111 +125,89 @@ def tile_picked_twostage_sigmoid_p_kernel(
                 raw.rearrange("p (j c i) -> p c j i", i=4, j=PACK),
             )
 
-        weave(nc.scalar.copy, w2_b[0], w2_raw[0])
-
-        sig_all = at("sig_all", PACK * S, F32, 0)
         sig = []
         for c in range(S // CHUNK):
-            bank = psum.tile([P, PACK * CHUNK], F32, name=f"score{c}", tag="chain")
+            bank = psum.tile([P, H], F32, name=f"score{c}", tag="a")
             cols = slice((c % 2) * CHUNK, (c % 2 + 1) * CHUNK)
-            for t in range(PACK):
-                nc.tensor.matmul_mx(
-                    out=bank[:, t * CHUNK : (t + 1) * CHUNK],
-                    lhsT=d_p[:, t * P : (t + 1) * P].bitcast(FP8X4),
-                    lhsT_scale=d_plane[:, t * P : (t + 1) * P],
-                    rhs=xq[c // 2][:, cols].bitcast(FP8X4),
-                    rhs_scale=xq_plane[:, c * CHUNK : (c + 1) * CHUNK],
-                    start=True,
-                    stop=True,
-                )
-            s_ = sig_all[:, c * PACK * CHUNK : (c + 1) * PACK * CHUNK]
+            nc.tensor.matmul_mx(
+                out=bank[:],
+                lhsT=xq[c // 2][:, cols].bitcast(FP8X4),
+                lhsT_scale=xq_plane[:, c * CHUNK : (c + 1) * CHUNK],
+                rhs=d_g[:].bitcast(FP8X4),
+                rhs_scale=d_plane[:],
+                start=True,
+                stop=True,
+            )
+            s_ = sb(f"sig{c}", H, F32)
             nc.scalar.activation(
-                s_.rearrange("p (j t) -> p j t", t=PACK),
-                bank[:].rearrange("p (t j) -> p j t", t=PACK),
+                s_[:].rearrange("j (t c i) -> j c t i", t=PACK, i=4),
+                bank[:].rearrange("j (c i t) -> j c t i", t=PACK, i=4),
                 SIGMOID,
                 scale=0.0625,
             )
             sig.append(s_)
 
-        gn_b = gn_t[:].unsqueeze(1).to_broadcast([P, CHUNK, PACK])
-        z_q = at("z_q", S, U32, 8192)
+        gn_b = gn_t[:].unsqueeze(1).unsqueeze(3).to_broadcast([P, CHUNK // 2, PACK, 2])
+        z_q = sb("z_q", S, U32)
         z_s = sb("z_s", S, U8)
         z_b = sb("z_b", PACK * S, BF16)
 
-        def weigh(c):
+        for c in range(S // CHUNK):
+            turned = psum.tile([P, PACK * CHUNK], F32, name=f"turned{c}", tag="b")
+            for t in range(PACK):
+                nc.tensor.transpose(
+                    turned[:, t * CHUNK : (t + 1) * CHUNK], sig[c][:, t * P : (t + 1) * P], ident[:]
+                )
             o = c * PACK * CHUNK
             nc.vector.tensor_tensor(
-                z_b[:, o : o + PACK * CHUNK].rearrange("p (j t) -> p j t", t=PACK),
-                sig[c].rearrange("p (j t) -> p j t", t=PACK),
+                z_b[:, o : o + PACK * CHUNK].rearrange("p (c i t) -> p c t i", t=PACK, i=2),
+                turned[:].rearrange("p (t c i) -> p c t i", t=PACK, i=2),
                 gn_b,
                 MULT,
             )
 
-        w1_first = sb("w1_first", PACK * 256, BF16)
-        w1_third = sb("w1_third", PACK * P, BF16)
         w2_q = [sb(f"w2_q{a}", 256, U32) for a in range(2)]
         w2_s = [sb(f"w2_s{a}", 256, U8) for a in range(2)]
-        w1_q = sb("w1_q", N, U32)
-        w1_s = sb("w1_s", N, U8)
+        w1_q = [sb(f"w1_q{a}", 256, U32) for a in range(2)]
+        w1_s = [sb(f"w1_s{a}", 256, U8) for a in range(2)]
         val = [sb(f"val{m}", S, F32) for m in range(N // P)]
         res = [sb(f"res{m}", S, F32) for m in range(N // P)]
 
         def quant(q, s, b):
             nc.vector.quantize_mx(q[:].bitcast(FP8X4), s[:], b[:])
 
-        def project(m):
-            bank = psum.tile([P, S], F32, name=f"valb{m}", tag="chain")
+        def product(m, bank, wq, ws, rq, rs):
             cols = slice((m % 2) * P, (m % 2 + 1) * P)
             nc.tensor.matmul_mx(
                 out=bank[:],
-                lhsT=w2_q[m // 2][:, cols].bitcast(FP8X4),
-                lhsT_scale=w2_s[m // 2][:, cols],
-                rhs=xo[:].bitcast(FP8X4),
-                rhs_scale=xo_plane[:],
+                lhsT=wq[m // 2][:, cols].bitcast(FP8X4),
+                lhsT_scale=ws[m // 2][:, cols],
+                rhs=rq[:].bitcast(FP8X4),
+                rhs_scale=rs[:],
                 start=True,
                 stop=True,
             )
+
+        def project(m):
+            bank = psum.tile([P, S], F32, name=f"valb{m}", tag="a")
+            product(m, bank, w2_q, w2_s, xo, xo_plane)
             nc.scalar.copy(val[m][:], bank[:])
 
         def finish(m):
-            bank = psum.tile([P, S], F32, name=f"h{m}", tag="h")
-            cols = slice(m * P, (m + 1) * P)
-            nc.tensor.matmul_mx(
-                out=bank[:],
-                lhsT=w1_q[:, cols].bitcast(FP8X4),
-                lhsT_scale=w1_s[:, cols],
-                rhs=z_q[:].bitcast(FP8X4),
-                rhs_scale=z_s[:],
-                start=True,
-                stop=True,
-            )
+            bank = psum.tile([P, S], F32, name=f"h{m}", tag="b")
+            product(m, bank, w1_q, w1_s, z_q, z_s)
             nc.vector.tensor_tensor(res[m][:], bank[:], val[m][:], MULT)
             nc.sync.dma_start(out[m * P : (m + 1) * P, :], res[m][:])
 
-        def weave_part(copy, dst, raw, lo, hi):
-            copy(
-                dst[:].rearrange("p (c i j) -> p c j i", i=4, j=PACK),
-                raw.rearrange("p (j c i) -> p c j i", i=4, j=PACK)[:, lo:hi],
-            )
-
-        def quant_w1(b, lo, hi):
-            nc.vector.quantize_mx(w1_q[:, lo:hi].bitcast(FP8X4), w1_s[:, lo:hi], b[:])
-
+        weave(nc.scalar.copy, w2_b[0], w2_raw[0])
         weave(nc.scalar.copy, w2_b[1], w2_raw[1])
-        weave(nc.scalar.copy, w1_first, w1_raw[0])
-        weave_part(nc.scalar.copy, w1_third, w1_raw[1], 0, 32)
-        weigh(0)
+        weave(nc.scalar.copy, w1_b[0], w1_raw[0])
+        weave(nc.scalar.copy, w1_b[1], w1_raw[1])
         quant(w2_q[0], w2_s[0], w2_b[0])
-        weigh(1)
-        weigh(2)
-        weigh(3)
         quant(w2_q[1], w2_s[1], w2_b[1])
         quant(z_q, z_s, z_b)
-        quant_w1(w1_first, 0, 256)
-        w1_last = sb("w1_last", PACK * P, BF16, "w1_first")
-        weave_part(nc.vector.tensor_copy, w1_last, w1_raw[1], 32, 64)
-        quant_w1(w1_third, 256, 384)
-        quant_w1(w1_last, 384, 512)
+        quant(w1_q[0], w1_s[0], w1_b[0])
+        quant(w1_q[1], w1_s[1], w1_b[1])
         for m in range(4):
             project(m)
         for m in range(4):

@@ -31,7 +31,7 @@ def tile_picked_twostage_sigmoid_p_kernel(
     with ExitStack() as ctx:
         keep = ctx.enter_context(tc.tile_pool(name="keep", bufs=1))
         placed = ctx.enter_context(tc.tile_pool(name="placed", bufs=1))
-        psum = ctx.enter_context(tc.psum_pool(name="psum", bufs=4))
+        psum = ctx.enter_context(tc.psum_pool(name="psum", bufs=1))
 
         def sb(name, width, dtype, slot=None):
             return keep.tile([P, width], dtype, name=name, tag=slot or name, align_bytes=64)
@@ -43,37 +43,31 @@ def tile_picked_twostage_sigmoid_p_kernel(
         offs_t = keep.tile([P, S // 16], U16, name="offs_t")
         own_t = keep.tile([P, S // 16], U16, name="own_t")
 
-        d_scale_win = sb("d_scale_win", G, U8)
+        d_scale_win = at("d_scale_win", G, U8, 0)
         x_scale_win = sb("x_scale_win", T, U8)
-        d_plane = sb("d_plane", H, U8)
+        score_planes = sb("score_planes", H + S, U8)
+        xo_plane = sb("xo_plane", S, U8)
         ident = sb("ident", P, F32)
-        nc.vector.memset(d_scale_win[:].bitcast(I32), 0)
         nc.vector.memset(x_scale_win[:].bitcast(I32), 0)
-        nc.vector.memset(d_plane[:].bitcast(I32), 0)
+        nc.vector.memset(d_scale_win[:].bitcast(I32), 0)
+        nc.vector.memset(score_planes[:].bitcast(I32), 0)
+        nc.vector.memset(xo_plane[:].bitcast(I32), 0)
         nc.vector.memset(ident[:], 0.0)
         make_identity(nc, ident[:], nomemset=True)
 
-        warm = sb("warm", 16, F32)
-        nc.gpsimd.memset(warm[:, 0:1], 0.0)
-        nc.scalar.activation(warm[:, 8:9], warm[:, 0:1], SIGMOID)
-
-        d_win = at("d_win", G, I32, 10240)
+        d_win = sb("d_win", G, I32)
         x_win = sb("x_win", T, I32)
         gn_t = sb("gn_t", PACK, F32)
 
-        nc.sync.dma_start(kidx_t[:], kidx)
+        nc.sync.dma_start(offs_t[:], offs)
         d_rows = d_words[0].rearrange("p c r -> p (c r)").bitcast(I32)
         nc.sync.dma_start(d_win[:, 0:512], d_rows[:, 0:512])
+        nc.sync.dma_start(x_scale_win[0:P:8, :].bitcast(I32), x_scales[0].bitcast(I32))
+        nc.sync.dma_start(kidx_t[:], kidx)
         nc.sync.dma_start(d_scale_win[0:P:8, :].bitcast(I32), d_scales[0].bitcast(I32))
-        nc.sync.dma_start(d_win[:, 512:G], d_rows[:, 512:G])
-        nc.sync.dma_start(offs_t[:], offs)
-        for q in range(4):
-            nc.sync.dma_start(
-                x_scale_win[32 * q : 32 * q + 4, :].bitcast(I32),
-                x_scales[0, 4 * q : 4 * q + 4, :].bitcast(I32),
-            )
-        nc.sync.dma_start(x_win[:], x_words[0].rearrange("p c r -> p (c r)").bitcast(I32))
         nc.sync.dma_start(own_t[:], own)
+        nc.sync.dma_start(d_win[:, 512:G], d_rows[:, 512:G])
+        nc.sync.dma_start(x_win[:], x_words[0].rearrange("p c r -> p (c r)").bitcast(I32))
 
         def load_w(w, raw, a):
             nc.sync.dma_start(
@@ -81,29 +75,34 @@ def tile_picked_twostage_sigmoid_p_kernel(
                 w.rearrange("(p j) n -> p j n", j=PACK)[:, :, a * 256 : (a + 1) * 256],
             )
 
-        w_first = at("w_first", PACK * 256, F32, 6144)
-        load_w(w2, [w_first[:]], 0)
-
-        d_scale_g = sb("d_scale_g", H, U8)
-        nc.vector.tensor_copy(d_scale_g[:], d_scale_win[:].indirect(kidx_t[:]))
-        for r in range(4):
-            nc.sync.dma_start(
-                d_plane[r:P:32, :].bitcast(I32),
-                d_scale_g[8 * r : P : 32, :].bitcast(I32),
-            )
         nc.sync.dma_start(gn_t[:], gn.rearrange("(p t) o -> p (t o)", t=PACK))
 
-        d_g = sb("d_g", H, U32)
-        nc.vector.tensor_copy(d_g[:], d_win[:].bitcast(U32).indirect(kidx_t[:]))
-        w_rest = at("w_rest", 3 * PACK * 256, F32, 10240)
-        w2_raw = [w_first[:], w_rest[:, 0:1024]]
-        w1_raw = [w_rest[:, a * 1024 : (a + 1) * 1024] for a in range(1, 3)]
+        def place(plane, spread):
+            for r in range(4):
+                nc.sync.dma_start(
+                    plane[r:P:32, :].bitcast(I32),
+                    spread[8 * r : P : 32, :].bitcast(I32),
+                )
+
+        score_g = sb("score_g", H + S, U8)
+        nc.vector.tensor_copy(score_g[:, H:], x_scale_win[:].indirect(offs_t[:]))
+        nc.vector.tensor_copy(score_g[:, :H], d_scale_win[:].indirect(kidx_t[:]))
+        place(score_planes, score_g)
+        d_plane = score_planes[:, :H]
+        xq_plane = score_planes[:, H:]
+        w_raw = at("w_raw", 4 * PACK * 256, F32, 0)
+        w2_raw = [w_raw[:, a * 1024 : (a + 1) * 1024] for a in range(2)]
+        w1_raw = [w_raw[:, a * 1024 : (a + 1) * 1024] for a in range(2, 4)]
+        load_w(w2, w2_raw, 0)
         load_w(w2, w2_raw, 1)
+        xo_g = sb("xo_g", S, U8)
+        nc.vector.tensor_copy(xo_g[:], x_scale_win[:].indirect(own_t[:]))
+        place(xo_plane, xo_g)
         load_w(w1, w1_raw, 0)
         load_w(w1, w1_raw, 1)
 
-        xq_plane = sb("xq_plane", S, U8)
-        nc.vector.tensor_copy(xq_plane[:], x_scale_win[:].indirect(offs_t[:]))
+        d_g = sb("d_g", H, U32)
+        nc.vector.tensor_copy(d_g[:], d_win[:].bitcast(U32).indirect(kidx_t[:]))
         xq = []
         for a in range(2):
             t_ = sb(f"xq{a}", HALF, U32)
@@ -111,8 +110,6 @@ def tile_picked_twostage_sigmoid_p_kernel(
                 t_[:], x_win[:].bitcast(U32).indirect(offs_t[:, a * 16 : (a + 1) * 16])
             )
             xq.append(t_)
-        xo_plane = sb("xo_plane", S, U8)
-        nc.vector.tensor_copy(xo_plane[:], x_scale_win[:].indirect(own_t[:]))
         xo = sb("xo", S, U32)
         nc.vector.tensor_copy(xo[:], x_win[:].bitcast(U32).indirect(own_t[:]))
 
@@ -125,22 +122,23 @@ def tile_picked_twostage_sigmoid_p_kernel(
                 raw.rearrange("p (j c i) -> p c j i", i=4, j=PACK),
             )
 
+        weave(nc.vector.tensor_copy, w2_b[0], w2_raw[0])
         sig = []
         for c in range(S // CHUNK):
-            bank = psum.tile([P, H], F32, name=f"score{c}", tag="a")
+            bank = psum.tile([P, H], F32, name=f"score{c}", offset=c * BANK)
             cols = slice((c % 2) * CHUNK, (c % 2 + 1) * CHUNK)
             nc.tensor.matmul_mx(
                 out=bank[:],
                 lhsT=xq[c // 2][:, cols].bitcast(FP8X4),
                 lhsT_scale=xq_plane[:, c * CHUNK : (c + 1) * CHUNK],
                 rhs=d_g[:].bitcast(FP8X4),
-                rhs_scale=d_plane[:],
+                rhs_scale=d_plane,
                 start=True,
                 stop=True,
             )
-            s_ = sb(f"sig{c}", H, F32)
+            s_ = at(f"sig{c}", H, F32, 16384 + c * 2048)[:]
             nc.scalar.activation(
-                s_[:].rearrange("j (t c i) -> j c t i", t=PACK, i=4),
+                s_.rearrange("j (t c i) -> j c t i", t=PACK, i=4),
                 bank[:].rearrange("j (c i t) -> j c t i", t=PACK, i=4),
                 SIGMOID,
                 scale=0.0625,
@@ -153,7 +151,7 @@ def tile_picked_twostage_sigmoid_p_kernel(
         z_b = sb("z_b", PACK * S, BF16)
 
         for c in range(S // CHUNK):
-            turned = psum.tile([P, PACK * CHUNK], F32, name=f"turned{c}", tag="b")
+            turned = psum.tile([P, PACK * CHUNK], F32, name=f"turned{c}", offset=(4 + c) * BANK)
             for t in range(PACK):
                 nc.tensor.transpose(
                     turned[:, t * CHUNK : (t + 1) * CHUNK], sig[c][:, t * P : (t + 1) * P], ident[:]
@@ -167,10 +165,11 @@ def tile_picked_twostage_sigmoid_p_kernel(
             )
 
         w2_q = [sb(f"w2_q{a}", 256, U32) for a in range(2)]
-        w2_s = [sb(f"w2_s{a}", 256, U8) for a in range(2)]
+        last_sig = 16384 + 3 * 2048
+        w2_s = [sb("w2_s0", 256, U8), at("w2_s1", 256, U8, last_sig)]
         w1_q = [sb(f"w1_q{a}", 256, U32) for a in range(2)]
-        w1_s = [sb(f"w1_s{a}", 256, U8) for a in range(2)]
-        val = [sb(f"val{m}", S, F32) for m in range(N // P)]
+        w1_s = [at(f"w1_s{a}", 256, U8, last_sig + 256 * (a + 1)) for a in range(2)]
+        val = [at(f"val{m}", S, F32, m * 2048) for m in range(N // P)]
         res = [sb(f"res{m}", S, F32) for m in range(N // P)]
 
         def quant(q, s, b):
@@ -189,17 +188,16 @@ def tile_picked_twostage_sigmoid_p_kernel(
             )
 
         def project(m):
-            bank = psum.tile([P, S], F32, name=f"valb{m}", tag="a")
+            bank = psum.tile([P, S], F32, name=f"valb{m}", offset=(3, 6, 0, 1)[m] * BANK)
             product(m, bank, w2_q, w2_s, xo, xo_plane)
             nc.scalar.copy(val[m][:], bank[:])
 
         def finish(m):
-            bank = psum.tile([P, S], F32, name=f"h{m}", tag="b")
+            bank = psum.tile([P, S], F32, name=f"h{m}", offset=(2, 4, 5, 7)[m] * BANK)
             product(m, bank, w1_q, w1_s, z_q, z_s)
             nc.vector.tensor_tensor(res[m][:], bank[:], val[m][:], MULT)
             nc.sync.dma_start(out[m * P : (m + 1) * P, :], res[m][:])
 
-        weave(nc.scalar.copy, w2_b[0], w2_raw[0])
         weave(nc.scalar.copy, w2_b[1], w2_raw[1])
         weave(nc.scalar.copy, w1_b[0], w1_raw[0])
         weave(nc.scalar.copy, w1_b[1], w1_raw[1])

@@ -22,6 +22,7 @@ PACK = 4
 HALF = S // 2
 CHUNK = 128
 BANK = 2048
+VECTOR_SHARE = 64
 
 
 def tile_picked_twostage_sigmoid_p_kernel(
@@ -43,8 +44,8 @@ def tile_picked_twostage_sigmoid_p_kernel(
         offs_t = keep.tile([P, S // 16], U16, name="offs_t")
         own_t = keep.tile([P, S // 16], U16, name="own_t")
 
-        d_scale_win = at("d_scale_win", G, U8, 0)
-        x_scale_win = sb("x_scale_win", T, U8)
+        d_scale_win = at("d_scale_win", G, U8, 3072)
+        x_scale_win = at("x_scale_win", T, U8, 11264)
         score_planes = sb("score_planes", H + S, U8)
         xo_plane = sb("xo_plane", S, U8)
         ident = sb("ident", P, F32)
@@ -59,9 +60,9 @@ def tile_picked_twostage_sigmoid_p_kernel(
         x_win = sb("x_win", T, I32)
         gn_t = sb("gn_t", PACK, F32)
 
-        nc.sync.dma_start(offs_t[:], offs)
         d_rows = d_words[0].rearrange("p c r -> p (c r)").bitcast(I32)
         nc.sync.dma_start(d_win[:, 0:512], d_rows[:, 0:512])
+        nc.sync.dma_start(offs_t[:], offs)
         nc.sync.dma_start(x_scale_win[0:P:8, :].bitcast(I32), x_scales[0].bitcast(I32))
         nc.sync.dma_start(kidx_t[:], kidx)
         nc.sync.dma_start(d_scale_win[0:P:8, :].bitcast(I32), d_scales[0].bitcast(I32))
@@ -90,53 +91,52 @@ def tile_picked_twostage_sigmoid_p_kernel(
         place(score_planes, score_g)
         d_plane = score_planes[:, :H]
         xq_plane = score_planes[:, H:]
-        w_raw = at("w_raw", 4 * PACK * 256, F32, 0)
-        w2_raw = [w_raw[:, a * 1024 : (a + 1) * 1024] for a in range(2)]
-        w1_raw = [w_raw[:, a * 1024 : (a + 1) * 1024] for a in range(2, 4)]
+        w2_raw = [at("w2_raw0", 1024, F32, 0)[:], at("w2_raw1", 1024, F32, 8192)[:]]
+        w1_raw = [at("w1_raw0", 1024, F32, 4096)[:], at("w1_raw1", 1536, F32, 12288)[:, :1024]]
         load_w(w2, w2_raw, 0)
-        load_w(w2, w2_raw, 1)
+        load_w(w1, w1_raw, 0)
         xo_g = sb("xo_g", S, U8)
         nc.vector.tensor_copy(xo_g[:], x_scale_win[:].indirect(own_t[:]))
         place(xo_plane, xo_g)
-        load_w(w1, w1_raw, 0)
+        load_w(w2, w2_raw, 1)
         load_w(w1, w1_raw, 1)
 
         d_g = sb("d_g", H, U32)
         nc.vector.tensor_copy(d_g[:], d_win[:].bitcast(U32).indirect(kidx_t[:]))
         xq = []
-        for a in range(2):
-            t_ = sb(f"xq{a}", HALF, U32)
+        for lo, hi in ((0, 1), (1, 2), (2, 4)):
+            t_ = sb(f"xq{lo}", (hi - lo) * CHUNK, U32)
             nc.vector.tensor_copy(
-                t_[:], x_win[:].bitcast(U32).indirect(offs_t[:, a * 16 : (a + 1) * 16])
+                t_[:], x_win[:].bitcast(U32).indirect(offs_t[:, lo * 8 : hi * 8])
             )
-            xq.append(t_)
+            xq.extend(t_[:, i * CHUNK : (i + 1) * CHUNK] for i in range(hi - lo))
         xo = sb("xo", S, U32)
         nc.vector.tensor_copy(xo[:], x_win[:].bitcast(U32).indirect(own_t[:]))
 
         w2_b = [sb("w2_b0", PACK * 256, BF16), sb("w2_b1", PACK * 256, BF16)]
-        w1_b = [sb("w1_b0", PACK * 256, BF16), sb("w1_b1", PACK * 256, BF16)]
+        w1_b = [sb("w1_b0", PACK * 256, BF16), at("w1_b1", PACK * 256, BF16, 18432 + 2 * 2048)]
 
-        def weave(copy, dst, raw):
+        def weave(copy, dst, raw, lo=0, hi=256):
+            groups = slice(lo // 4, hi // 4)
             copy(
-                dst[:].rearrange("p (c i j) -> p c j i", i=4, j=PACK),
-                raw.rearrange("p (j c i) -> p c j i", i=4, j=PACK),
+                dst[:].rearrange("p (c i j) -> p c j i", i=4, j=PACK)[:, groups],
+                raw.rearrange("p (j c i) -> p c j i", i=4, j=PACK)[:, groups],
             )
 
         weave(nc.vector.tensor_copy, w2_b[0], w2_raw[0])
         sig = []
         for c in range(S // CHUNK):
             bank = psum.tile([P, H], F32, name=f"score{c}", offset=c * BANK)
-            cols = slice((c % 2) * CHUNK, (c % 2 + 1) * CHUNK)
             nc.tensor.matmul_mx(
                 out=bank[:],
-                lhsT=xq[c // 2][:, cols].bitcast(FP8X4),
+                lhsT=xq[c].bitcast(FP8X4),
                 lhsT_scale=xq_plane[:, c * CHUNK : (c + 1) * CHUNK],
                 rhs=d_g[:].bitcast(FP8X4),
                 rhs_scale=d_plane,
                 start=True,
                 stop=True,
             )
-            s_ = at(f"sig{c}", H, F32, 16384 + c * 2048)[:]
+            s_ = at(f"sig{c}", H, F32, 18432 + c * 2048)[:]
             nc.scalar.activation(
                 s_.rearrange("j (t c i) -> j c t i", t=PACK, i=4),
                 bank[:].rearrange("j (c i t) -> j c t i", t=PACK, i=4),
@@ -165,11 +165,11 @@ def tile_picked_twostage_sigmoid_p_kernel(
             )
 
         w2_q = [sb(f"w2_q{a}", 256, U32) for a in range(2)]
-        last_sig = 16384 + 3 * 2048
+        last_sig = 18432 + 3 * 2048
         w2_s = [sb("w2_s0", 256, U8), at("w2_s1", 256, U8, last_sig)]
         w1_q = [sb(f"w1_q{a}", 256, U32) for a in range(2)]
         w1_s = [at(f"w1_s{a}", 256, U8, last_sig + 256 * (a + 1)) for a in range(2)]
-        val = [at(f"val{m}", S, F32, m * 2048) for m in range(N // P)]
+        val = [at(f"val{m}", S, F32, 10240 + m * 2048) for m in range(N // P)]
         res = [sb(f"res{m}", S, F32) for m in range(N // P)]
 
         def quant(q, s, b):
@@ -198,13 +198,23 @@ def tile_picked_twostage_sigmoid_p_kernel(
             nc.vector.tensor_tensor(res[m][:], bank[:], val[m][:], MULT)
             nc.sync.dma_start(out[m * P : (m + 1) * P, :], res[m][:])
 
-        weave(nc.scalar.copy, w2_b[1], w2_raw[1])
-        weave(nc.scalar.copy, w1_b[0], w1_raw[0])
-        weave(nc.scalar.copy, w1_b[1], w1_raw[1])
+        def quant_z(a):
+            cols = slice(a * HALF, (a + 1) * HALF)
+            nc.vector.quantize_mx(
+                z_q[:, cols].bitcast(FP8X4),
+                z_s[:, cols],
+                z_b[:, a * PACK * HALF : (a + 1) * PACK * HALF],
+            )
+
         quant(w2_q[0], w2_s[0], w2_b[0])
-        quant(w2_q[1], w2_s[1], w2_b[1])
-        quant(z_q, z_s, z_b)
+        weave(nc.scalar.copy, w1_b[0], w1_raw[0])
+        weave(nc.scalar.copy, w2_b[1], w2_raw[1])
         quant(w1_q[0], w1_s[0], w1_b[0])
+        quant_z(0)
+        quant_z(1)
+        weave(nc.scalar.copy, w1_b[1], w1_raw[1], 0, 256 - VECTOR_SHARE)
+        weave(nc.vector.tensor_copy, w1_b[1], w1_raw[1], 256 - VECTOR_SHARE, 256)
+        quant(w2_q[1], w2_s[1], w2_b[1])
         quant(w1_q[1], w1_s[1], w1_b[1])
         for m in range(4):
             project(m)

@@ -22,7 +22,6 @@ PACK = 4
 HALF = S // 2
 CHUNK = 128
 BANK = 2048
-VECTOR_SHARE = 64
 
 
 def tile_picked_twostage_sigmoid_p_kernel(
@@ -91,14 +90,14 @@ def tile_picked_twostage_sigmoid_p_kernel(
         place(score_planes, score_g)
         d_plane = score_planes[:, :H]
         xq_plane = score_planes[:, H:]
-        w2_raw = [at("w2_raw0", 1024, F32, 0)[:], at("w2_raw1", 1024, F32, 8192)[:]]
-        w1_raw = [at("w1_raw0", 1024, F32, 4096)[:], at("w1_raw1", 1536, F32, 12288)[:, :1024]]
+        w2_raw = [at("w2_raw0", 1024, F32, 0)[:], at("w2_raw1", 1024, F32, 4096)[:]]
+        w1_raw = [at("w1_raw0", 1024, F32, 8192)[:], at("w1_raw1", 1536, F32, 12288)[:, :1024]]
         load_w(w2, w2_raw, 0)
-        load_w(w1, w1_raw, 0)
+        load_w(w2, w2_raw, 1)
         xo_g = sb("xo_g", S, U8)
         nc.vector.tensor_copy(xo_g[:], x_scale_win[:].indirect(own_t[:]))
         place(xo_plane, xo_g)
-        load_w(w2, w2_raw, 1)
+        load_w(w1, w1_raw, 0)
         load_w(w1, w1_raw, 1)
 
         d_g = sb("d_g", H, U32)
@@ -114,7 +113,7 @@ def tile_picked_twostage_sigmoid_p_kernel(
         nc.vector.tensor_copy(xo[:], x_win[:].bitcast(U32).indirect(own_t[:]))
 
         w2_b = [sb("w2_b0", PACK * 256, BF16), sb("w2_b1", PACK * 256, BF16)]
-        w1_b = [sb("w1_b0", PACK * 256, BF16), at("w1_b1", PACK * 256, BF16, 18432 + 2 * 2048)]
+        w1_b = [sb("w1_b0", PACK * 256, BF16), sb("w1_b1", PACK * 256, BF16)]
 
         def weave(copy, dst, raw, lo=0, hi=256):
             groups = slice(lo // 4, hi // 4)
@@ -136,7 +135,7 @@ def tile_picked_twostage_sigmoid_p_kernel(
                 start=True,
                 stop=True,
             )
-            s_ = at(f"sig{c}", H, F32, 18432 + c * 2048)[:]
+            s_ = at(f"sig{c}", H, F32, 20480 + c * 2048)[:]
             nc.scalar.activation(
                 s_.rearrange("j (t c i) -> j c t i", t=PACK, i=4),
                 bank[:].rearrange("j (c i t) -> j c t i", t=PACK, i=4),
@@ -165,7 +164,7 @@ def tile_picked_twostage_sigmoid_p_kernel(
             )
 
         w2_q = [sb(f"w2_q{a}", 256, U32) for a in range(2)]
-        last_sig = 18432 + 3 * 2048
+        last_sig = 20480 + 3 * 2048
         w2_s = [sb("w2_s0", 256, U8), at("w2_s1", 256, U8, last_sig)]
         w1_q = [sb(f"w1_q{a}", 256, U32) for a in range(2)]
         w1_s = [at(f"w1_s{a}", 256, U8, last_sig + 256 * (a + 1)) for a in range(2)]
@@ -175,14 +174,14 @@ def tile_picked_twostage_sigmoid_p_kernel(
         def quant(q, s, b):
             nc.vector.quantize_mx(q[:].bitcast(FP8X4), s[:], b[:])
 
-        def product(m, bank, wq, ws, rq, rs):
+        def product(m, bank, wq, ws, rq, rs, part=slice(0, S)):
             cols = slice((m % 2) * P, (m % 2 + 1) * P)
             nc.tensor.matmul_mx(
-                out=bank[:],
+                out=bank[:, part],
                 lhsT=wq[m // 2][:, cols].bitcast(FP8X4),
                 lhsT_scale=ws[m // 2][:, cols],
-                rhs=rq[:].bitcast(FP8X4),
-                rhs_scale=rs[:],
+                rhs=rq[:, part].bitcast(FP8X4),
+                rhs_scale=rs[:, part],
                 start=True,
                 stop=True,
             )
@@ -192,10 +191,19 @@ def tile_picked_twostage_sigmoid_p_kernel(
             product(m, bank, w2_q, w2_s, xo, xo_plane)
             nc.scalar.copy(val[m][:], bank[:])
 
+        halves = (slice(0, HALF), slice(HALF, S))
+
         def finish(m):
-            bank = psum.tile([P, S], F32, name=f"h{m}", offset=(2, 4, 5, 7)[m] * BANK)
-            product(m, bank, w1_q, w1_s, z_q, z_s)
-            nc.vector.tensor_tensor(res[m][:], bank[:], val[m][:], MULT)
+            if m == 0:
+                for a, part in enumerate(halves):
+                    bank = psum.tile([P, S], F32, name=f"h0_{a}", offset=(2, 4)[a] * BANK)
+                    product(m, bank, w1_q, w1_s, z_q, z_s, part)
+                    nc.vector.tensor_tensor(res[m][:, part], bank[:, part], val[m][:, part], MULT)
+            else:
+                bank = psum.tile([P, S], F32, name=f"h{m}", offset=(None, 5, 7, 3)[m] * BANK)
+                for part in halves if m == 1 else (slice(0, S),):
+                    product(m, bank, w1_q, w1_s, z_q, z_s, part)
+                nc.vector.tensor_tensor(res[m][:], bank[:], val[m][:], MULT)
             nc.sync.dma_start(out[m * P : (m + 1) * P, :], res[m][:])
 
         def quant_z(a):
@@ -207,14 +215,13 @@ def tile_picked_twostage_sigmoid_p_kernel(
             )
 
         quant(w2_q[0], w2_s[0], w2_b[0])
-        weave(nc.scalar.copy, w1_b[0], w1_raw[0])
         weave(nc.scalar.copy, w2_b[1], w2_raw[1])
+        weave(nc.scalar.copy, w1_b[0], w1_raw[0])
+        weave(nc.scalar.copy, w1_b[1], w1_raw[1])
+        quant(w2_q[1], w2_s[1], w2_b[1])
         quant(w1_q[0], w1_s[0], w1_b[0])
         quant_z(0)
         quant_z(1)
-        weave(nc.scalar.copy, w1_b[1], w1_raw[1], 0, 256 - VECTOR_SHARE)
-        weave(nc.vector.tensor_copy, w1_b[1], w1_raw[1], 256 - VECTOR_SHARE, 256)
-        quant(w2_q[1], w2_s[1], w2_b[1])
         quant(w1_q[1], w1_s[1], w1_b[1])
         for m in range(4):
             project(m)

@@ -65,8 +65,8 @@ def tile_picked_twostage_sigmoid_p_kernel(
         nc.sync.dma_start(x_scale_win[0:P:8, :].bitcast(I32), x_scales[0].bitcast(I32))
         nc.sync.dma_start(kidx_t[:], kidx)
         nc.sync.dma_start(d_scale_win[0:P:8, :].bitcast(I32), d_scales[0].bitcast(I32))
-        nc.sync.dma_start(own_t[:], own)
         nc.sync.dma_start(d_win[:, 512:G], d_rows[:, 512:G])
+        nc.sync.dma_start(own_t[:], own)
         nc.sync.dma_start(x_win[:], x_words[0].rearrange("p c r -> p (c r)").bitcast(I32))
 
         def load_w(w, raw, a):
@@ -90,18 +90,18 @@ def tile_picked_twostage_sigmoid_p_kernel(
         place(score_planes, score_g)
         d_plane = score_planes[:, :H]
         xq_plane = score_planes[:, H:]
-        w2_raw = [at("w2_raw0", 1024, F32, 0)[:], at("w2_raw1", 1024, F32, 4096)[:]]
+        w2_whole = at("w2_whole", 2048, F32, 0)
+        nc.sync.dma_start(w2_whole[:], w2.rearrange("(p j) n -> p (j n)", j=PACK))
+        w2_raw = w2_whole[:].rearrange("p (j n) -> p j n", j=PACK)
         w1_raw = [at("w1_raw0", 1024, F32, 8192)[:], at("w1_raw1", 1536, F32, 12288)[:, :1024]]
-        load_w(w2, w2_raw, 0)
-        load_w(w2, w2_raw, 1)
+        d_g = sb("d_g", H, U32)
+        nc.vector.tensor_copy(d_g[:], d_win[:].bitcast(U32).indirect(kidx_t[:]))
         xo_g = sb("xo_g", S, U8)
         nc.vector.tensor_copy(xo_g[:], x_scale_win[:].indirect(own_t[:]))
         place(xo_plane, xo_g)
         load_w(w1, w1_raw, 0)
         load_w(w1, w1_raw, 1)
 
-        d_g = sb("d_g", H, U32)
-        nc.vector.tensor_copy(d_g[:], d_win[:].bitcast(U32).indirect(kidx_t[:]))
         xq = []
         for lo, hi in ((0, 1), (1, 2), (2, 4)):
             t_ = sb(f"xq{lo}", (hi - lo) * CHUNK, U32)
@@ -115,13 +115,14 @@ def tile_picked_twostage_sigmoid_p_kernel(
         w2_b = [sb("w2_b0", PACK * 256, BF16), sb("w2_b1", PACK * 256, BF16)]
         w1_b = [sb("w1_b0", PACK * 256, BF16), sb("w1_b1", PACK * 256, BF16)]
 
-        def weave(copy, dst, raw, lo=0, hi=256):
-            groups = slice(lo // 4, hi // 4)
+        def weave(copy, dst, rows):
             copy(
-                dst[:].rearrange("p (c i j) -> p c j i", i=4, j=PACK)[:, groups],
-                raw.rearrange("p (j c i) -> p c j i", i=4, j=PACK)[:, groups],
+                dst[:].rearrange("p (c i j) -> p c j i", i=4, j=PACK),
+                rows.rearrange("p j (c i) -> p c j i", i=4),
             )
 
+        w1_raw = [raw.rearrange("p (j n) -> p j n", j=PACK) for raw in w1_raw]
+        w2_raw = [w2_raw[:, :, a * 256 : (a + 1) * 256] for a in range(2)]
         weave(nc.vector.tensor_copy, w2_b[0], w2_raw[0])
         sig = []
         for c in range(S // CHUNK):
@@ -186,12 +187,13 @@ def tile_picked_twostage_sigmoid_p_kernel(
                 stop=True,
             )
 
+        halves = (slice(0, HALF), slice(HALF, S))
+
         def project(m):
             bank = psum.tile([P, S], F32, name=f"valb{m}", offset=(3, 6, 0, 1)[m] * BANK)
             product(m, bank, w2_q, w2_s, xo, xo_plane)
-            nc.scalar.copy(val[m][:], bank[:])
-
-        halves = (slice(0, HALF), slice(HALF, S))
+            for part in halves if m == 3 else (slice(0, S),):
+                nc.scalar.copy(val[m][:, part], bank[:, part])
 
         def finish(m):
             if m == 0:
@@ -203,7 +205,8 @@ def tile_picked_twostage_sigmoid_p_kernel(
                 bank = psum.tile([P, S], F32, name=f"h{m}", offset=(None, 5, 7, 3)[m] * BANK)
                 for part in halves if m == 1 else (slice(0, S),):
                     product(m, bank, w1_q, w1_s, z_q, z_s, part)
-                nc.vector.tensor_tensor(res[m][:], bank[:], val[m][:], MULT)
+                for part in halves if m == 3 else (slice(0, S),):
+                    nc.vector.tensor_tensor(res[m][:, part], bank[:, part], val[m][:, part], MULT)
             nc.sync.dma_start(out[m * P : (m + 1) * P, :], res[m][:])
 
         def quant_z(a):

@@ -147,10 +147,25 @@ def tile_picked_twostage_sigmoid_p_kernel(
 
         gn_b = gn_t[:].unsqueeze(1).unsqueeze(3).to_broadcast([P, CHUNK // 2, PACK, 2])
         z_q = sb("z_q", S, U32)
-        z_s = sb("z_s", S, U8)
+        z_s = at("z_s", S, U8, 20480 + 2 * 2048)
         z_b = sb("z_b", PACK * S, BF16)
 
+        w2_q = [sb(f"w2_q{a}", 256, U32) for a in range(2)]
+        last_sig = 20480 + 3 * 2048
+        w2_s = [sb("w2_s0", 256, U8), sb("w2_s1", 256, U8)]
+        w1_q = [sb(f"w1_q{a}", 256, U32) for a in range(2)]
+        w1_s = [at(f"w1_s{a}", 256, U8, last_sig + 256 * (a + 1)) for a in range(2)]
+        val = [at(f"val{m}", S, F32, 10240 + m * 2048) for m in range(N // P)]
+        res = [sb(f"res{m}", S, F32) for m in range(N // P)]
+
+        def quant(q, s, b):
+            nc.vector.quantize_mx(q[:].bitcast(FP8X4), s[:], b[:])
+
+        quant(w2_q[0], w2_s[0], w2_b[0])
+        weave(nc.scalar.copy, w2_b[1], w2_raw[1])
         for c in range(S // CHUNK):
+            if c == 2:
+                quant(w2_q[1], w2_s[1], w2_b[1])
             turned = psum.tile([P, PACK * CHUNK], F32, name=f"turned{c}", offset=(4 + c) * BANK)
             for t in range(PACK):
                 nc.tensor.transpose(
@@ -163,17 +178,6 @@ def tile_picked_twostage_sigmoid_p_kernel(
                 gn_b,
                 MULT,
             )
-
-        w2_q = [sb(f"w2_q{a}", 256, U32) for a in range(2)]
-        last_sig = 20480 + 3 * 2048
-        w2_s = [sb("w2_s0", 256, U8), at("w2_s1", 256, U8, last_sig)]
-        w1_q = [sb(f"w1_q{a}", 256, U32) for a in range(2)]
-        w1_s = [at(f"w1_s{a}", 256, U8, last_sig + 256 * (a + 1)) for a in range(2)]
-        val = [at(f"val{m}", S, F32, 10240 + m * 2048) for m in range(N // P)]
-        res = [sb(f"res{m}", S, F32) for m in range(N // P)]
-
-        def quant(q, s, b):
-            nc.vector.quantize_mx(q[:].bitcast(FP8X4), s[:], b[:])
 
         def product(m, bank, wq, ws, rq, rs, part=slice(0, S)):
             cols = slice((m % 2) * P, (m % 2 + 1) * P)
@@ -190,7 +194,7 @@ def tile_picked_twostage_sigmoid_p_kernel(
         halves = (slice(0, HALF), slice(HALF, S))
 
         def project(m):
-            bank = psum.tile([P, S], F32, name=f"valb{m}", offset=(3, 6, 0, 1)[m] * BANK)
+            bank = psum.tile([P, S], F32, name=f"valb{m}", offset=(2, 3, 0, 1)[m] * BANK)
             product(m, bank, w2_q, w2_s, xo, xo_plane)
             for part in halves if m == 3 else (slice(0, S),):
                 nc.scalar.copy(val[m][:, part], bank[:, part])
@@ -198,33 +202,30 @@ def tile_picked_twostage_sigmoid_p_kernel(
         def finish(m):
             if m == 0:
                 for a, part in enumerate(halves):
-                    bank = psum.tile([P, S], F32, name=f"h0_{a}", offset=(2, 4)[a] * BANK)
+                    bank = psum.tile([P, S], F32, name=f"h0_{a}", offset=(6, 4)[a] * BANK)
                     product(m, bank, w1_q, w1_s, z_q, z_s, part)
                     nc.vector.tensor_tensor(res[m][:, part], bank[:, part], val[m][:, part], MULT)
             else:
-                bank = psum.tile([P, S], F32, name=f"h{m}", offset=(None, 5, 7, 3)[m] * BANK)
-                for part in halves if m == 1 else (slice(0, S),):
-                    product(m, bank, w1_q, w1_s, z_q, z_s, part)
+                bank = psum.tile([P, S], F32, name=f"h{m}", offset=(None, 5, 7, 2)[m] * BANK)
+                product(m, bank, w1_q, w1_s, z_q, z_s)
                 for part in halves if m == 3 else (slice(0, S),):
                     nc.vector.tensor_tensor(res[m][:, part], bank[:, part], val[m][:, part], MULT)
             nc.sync.dma_start(out[m * P : (m + 1) * P, :], res[m][:])
 
-        def quant_z(a):
-            cols = slice(a * HALF, (a + 1) * HALF)
+        def quant_z(lo, hi):
+            cols = slice(lo * CHUNK, hi * CHUNK)
             nc.vector.quantize_mx(
                 z_q[:, cols].bitcast(FP8X4),
                 z_s[:, cols],
-                z_b[:, a * PACK * HALF : (a + 1) * PACK * HALF],
+                z_b[:, lo * PACK * CHUNK : hi * PACK * CHUNK],
             )
 
-        quant(w2_q[0], w2_s[0], w2_b[0])
-        weave(nc.scalar.copy, w2_b[1], w2_raw[1])
         weave(nc.scalar.copy, w1_b[0], w1_raw[0])
         weave(nc.scalar.copy, w1_b[1], w1_raw[1])
-        quant(w2_q[1], w2_s[1], w2_b[1])
         quant(w1_q[0], w1_s[0], w1_b[0])
-        quant_z(0)
-        quant_z(1)
+        quant_z(0, 2)
+        quant_z(2, 3)
+        quant_z(3, 4)
         quant(w1_q[1], w1_s[1], w1_b[1])
         for m in range(4):
             project(m)

@@ -15,13 +15,31 @@ U8 = mybir.dt.uint8
 FP8X4 = mybir.dt.float8_e4m3fn_x4
 SIGMOID = mybir.ActivationFunctionType.Sigmoid
 MULT = mybir.AluOpType.mult
-ADD = mybir.AluOpType.add
 
 P = 128
 PACK = 4
-HALF = S // 2
+LIST_ROWS = 16
 CHUNK = 128
+HALF = S // 2
+W_HALF = N // 2
+RUN = 4
 BANK = 2048
+
+D_HEAD = G // 4
+VECTOR_SHARE = 64
+
+ROW_BYTES = S * 4
+W2_AT = 0
+D_SCALE_AT = 3072
+W1_AT = (8192, 12288)
+X_SCALE_AT = 11264
+VAL_AT = 10240
+SIG_AT = 20480
+LAST_SIG_AT = SIG_AT + 3 * ROW_BYTES
+
+VAL_BANKS = (2, 3, 0, 1)
+H0_BANKS = (6, 4)
+H_BANKS = {1: 5, 2: 7, 3: 2}
 
 
 def tile_picked_twostage_sigmoid_p_kernel(
@@ -33,18 +51,18 @@ def tile_picked_twostage_sigmoid_p_kernel(
         placed = ctx.enter_context(tc.tile_pool(name="placed", bufs=1))
         psum = ctx.enter_context(tc.psum_pool(name="psum", bufs=1))
 
-        def sb(name, width, dtype, slot=None):
-            return keep.tile([P, width], dtype, name=name, tag=slot or name, align_bytes=64)
+        def sb(name, width, dtype):
+            return keep.tile([P, width], dtype, name=name, tag=name, align_bytes=64)
 
         def at(name, width, dtype, offset):
             return placed.tile([P, width], dtype, name=name, align_bytes=64, offset=offset)
 
-        kidx_t = keep.tile([P, H // 16], U16, name="kidx_t")
-        offs_t = keep.tile([P, S // 16], U16, name="offs_t")
-        own_t = keep.tile([P, S // 16], U16, name="own_t")
+        kidx_t = keep.tile([P, H // LIST_ROWS], U16, name="kidx_t")
+        offs_t = keep.tile([P, S // LIST_ROWS], U16, name="offs_t")
+        own_t = keep.tile([P, S // LIST_ROWS], U16, name="own_t")
 
-        d_scale_win = at("d_scale_win", G, U8, 3072)
-        x_scale_win = at("x_scale_win", T, U8, 11264)
+        d_scale_win = at("d_scale_win", G, U8, D_SCALE_AT)
+        x_scale_win = at("x_scale_win", T, U8, X_SCALE_AT)
         score_planes = sb("score_planes", H + S, U8)
         xo_plane = sb("xo_plane", S, U8)
         ident = sb("ident", P, F32)
@@ -60,21 +78,14 @@ def tile_picked_twostage_sigmoid_p_kernel(
         gn_t = sb("gn_t", PACK, F32)
 
         d_rows = d_words[0].rearrange("p c r -> p (c r)").bitcast(I32)
-        nc.sync.dma_start(d_win[:, 0:512], d_rows[:, 0:512])
+        nc.sync.dma_start(d_win[:, 0:D_HEAD], d_rows[:, 0:D_HEAD])
         nc.sync.dma_start(offs_t[:], offs)
         nc.sync.dma_start(x_scale_win[0:P:8, :].bitcast(I32), x_scales[0].bitcast(I32))
         nc.sync.dma_start(kidx_t[:], kidx)
         nc.sync.dma_start(d_scale_win[0:P:8, :].bitcast(I32), d_scales[0].bitcast(I32))
-        nc.sync.dma_start(d_win[:, 512:G], d_rows[:, 512:G])
+        nc.sync.dma_start(d_win[:, D_HEAD:G], d_rows[:, D_HEAD:G])
         nc.sync.dma_start(own_t[:], own)
         nc.sync.dma_start(x_win[:], x_words[0].rearrange("p c r -> p (c r)").bitcast(I32))
-
-        def load_w(w, raw, a):
-            nc.sync.dma_start(
-                raw[a].rearrange("p (j n) -> p j n", j=PACK),
-                w.rearrange("(p j) n -> p j n", j=PACK)[:, :, a * 256 : (a + 1) * 256],
-            )
-
         nc.sync.dma_start(gn_t[:], gn.rearrange("(p t) o -> p (t o)", t=PACK))
 
         def place(plane, spread):
@@ -90,45 +101,58 @@ def tile_picked_twostage_sigmoid_p_kernel(
         place(score_planes, score_g)
         d_plane = score_planes[:, :H]
         xq_plane = score_planes[:, H:]
-        w2_whole = at("w2_whole", 2048, F32, 0)
+
+        w2_whole = at("w2_whole", PACK * N, F32, W2_AT)
         nc.sync.dma_start(w2_whole[:], w2.rearrange("(p j) n -> p (j n)", j=PACK))
-        w2_raw = w2_whole[:].rearrange("p (j n) -> p j n", j=PACK)
-        w1_raw = [at("w1_raw0", 1024, F32, 8192)[:], at("w1_raw1", 1536, F32, 12288)[:, :1024]]
+        w2_rows = w2_whole[:].rearrange("p (j n) -> p j n", j=PACK)
+        w2_raw = [w2_rows[:, :, a * W_HALF : (a + 1) * W_HALF] for a in range(2)]
+        w1_flat = [
+            at("w1_raw0", PACK * W_HALF, F32, W1_AT[0])[:],
+            at("w1_raw1", 3 * S, F32, W1_AT[1])[:, : PACK * W_HALF],
+        ]
+        w1_raw = [flat.rearrange("p (j n) -> p j n", j=PACK) for flat in w1_flat]
+
         d_g = sb("d_g", H, U32)
         nc.vector.tensor_copy(d_g[:], d_win[:].bitcast(U32).indirect(kidx_t[:]))
         xo_g = sb("xo_g", S, U8)
         nc.vector.tensor_copy(xo_g[:], x_scale_win[:].indirect(own_t[:]))
         place(xo_plane, xo_g)
-        load_w(w1, w1_raw, 0)
-        load_w(w1, w1_raw, 1)
+        w1_rows = w1.rearrange("(p j) n -> p j n", j=PACK)
+        for a in range(2):
+            nc.sync.dma_start(w1_raw[a], w1_rows[:, :, a * W_HALF : (a + 1) * W_HALF])
 
         xq = []
+        list_cols = CHUNK // LIST_ROWS
         for lo, hi in ((0, 1), (1, 2), (2, 4)):
-            t_ = sb(f"xq{lo}", (hi - lo) * CHUNK, U32)
+            piece = sb(f"xq{lo}", (hi - lo) * CHUNK, U32)
             nc.vector.tensor_copy(
-                t_[:], x_win[:].bitcast(U32).indirect(offs_t[:, lo * 8 : hi * 8])
+                piece[:], x_win[:].bitcast(U32).indirect(offs_t[:, lo * list_cols : hi * list_cols])
             )
-            xq.extend(t_[:, i * CHUNK : (i + 1) * CHUNK] for i in range(hi - lo))
+            xq.extend(piece[:, i * CHUNK : (i + 1) * CHUNK] for i in range(hi - lo))
         xo = sb("xo", S, U32)
         nc.vector.tensor_copy(xo[:], x_win[:].bitcast(U32).indirect(own_t[:]))
 
-        w2_b = [sb("w2_b0", PACK * 256, BF16), sb("w2_b1", PACK * 256, BF16)]
-        w1_b = [sb("w1_b0", PACK * 256, BF16), sb("w1_b1", PACK * 256, BF16)]
+        w2_b = [sb(f"w2_b{a}", PACK * W_HALF, BF16) for a in range(2)]
+        w1_b = [sb(f"w1_b{a}", PACK * W_HALF, BF16) for a in range(2)]
 
         def weave(copy, dst, rows):
             copy(
-                dst[:].rearrange("p (c i j) -> p c j i", i=4, j=PACK),
-                rows.rearrange("p j (c i) -> p c j i", i=4),
+                dst.rearrange("p (c i j) -> p c j i", i=RUN, j=PACK),
+                rows.rearrange("p j (c i) -> p c j i", i=RUN),
             )
 
-        w1_raw = [raw.rearrange("p (j n) -> p j n", j=PACK) for raw in w1_raw]
-        w2_raw = [w2_raw[:, :, a * 256 : (a + 1) * 256] for a in range(2)]
-        weave(nc.vector.tensor_copy, w2_b[0], w2_raw[0])
+        weave(nc.vector.tensor_copy, w2_b[0][:], w2_raw[0])
+        weave(
+            nc.vector.tensor_copy,
+            w2_b[1][:, : PACK * VECTOR_SHARE],
+            w2_raw[1][:, :, :VECTOR_SHARE],
+        )
+
         sig = []
         for c in range(S // CHUNK):
-            bank = psum.tile([P, H], F32, name=f"score{c}", offset=c * BANK)
+            scores = psum.tile([P, H], F32, name=f"score{c}", offset=c * BANK)
             nc.tensor.matmul_mx(
-                out=bank[:],
+                out=scores[:],
                 lhsT=xq[c].bitcast(FP8X4),
                 lhsT_scale=xq_plane[:, c * CHUNK : (c + 1) * CHUNK],
                 rhs=d_g[:].bitcast(FP8X4),
@@ -136,98 +160,92 @@ def tile_picked_twostage_sigmoid_p_kernel(
                 start=True,
                 stop=True,
             )
-            s_ = at(f"sig{c}", H, F32, 20480 + c * 2048)[:]
+            sig.append(at(f"sig{c}", H, F32, SIG_AT + c * ROW_BYTES)[:])
             nc.scalar.activation(
-                s_.rearrange("j (t c i) -> j c t i", t=PACK, i=4),
-                bank[:].rearrange("j (c i t) -> j c t i", t=PACK, i=4),
+                sig[c].rearrange("j (t g i) -> j g t i", t=PACK, i=RUN),
+                scores[:].rearrange("j (g i t) -> j g t i", t=PACK, i=RUN),
                 SIGMOID,
                 scale=0.0625,
             )
-            sig.append(s_)
 
         gn_b = gn_t[:].unsqueeze(1).unsqueeze(3).to_broadcast([P, CHUNK // 2, PACK, 2])
         z_q = sb("z_q", S, U32)
-        z_s = at("z_s", S, U8, 20480 + 2 * 2048)
+        z_s = at("z_s", S, U8, LAST_SIG_AT + 4 * W_HALF)
         z_b = sb("z_b", PACK * S, BF16)
-
-        w2_q = [sb(f"w2_q{a}", 256, U32) for a in range(2)]
-        last_sig = 20480 + 3 * 2048
-        w2_s = [sb("w2_s0", 256, U8), sb("w2_s1", 256, U8)]
-        w1_q = [sb(f"w1_q{a}", 256, U32) for a in range(2)]
-        w1_s = [at(f"w1_s{a}", 256, U8, last_sig + 256 * (a + 1)) for a in range(2)]
-        val = [at(f"val{m}", S, F32, 10240 + m * 2048) for m in range(N // P)]
+        w2_q = [sb(f"w2_q{a}", W_HALF, U32) for a in range(2)]
+        w2_s = [sb(f"w2_s{a}", W_HALF, U8) for a in range(2)]
+        w1_q = [sb(f"w1_q{a}", W_HALF, U32) for a in range(2)]
+        w1_s = [at(f"w1_s{a}", W_HALF, U8, LAST_SIG_AT + W_HALF * (a + 1)) for a in range(2)]
+        val = [at(f"val{m}", S, F32, VAL_AT + m * ROW_BYTES) for m in range(N // P)]
         res = [sb(f"res{m}", S, F32) for m in range(N // P)]
 
-        def quant(q, s, b):
-            nc.vector.quantize_mx(q[:].bitcast(FP8X4), s[:], b[:])
+        def quant(codes, plane, woven):
+            nc.vector.quantize_mx(codes.bitcast(FP8X4), plane, woven)
 
-        quant(w2_q[0], w2_s[0], w2_b[0])
-        weave(nc.scalar.copy, w2_b[1], w2_raw[1])
-        for c in range(S // CHUNK):
-            if c == 2:
-                quant(w2_q[1], w2_s[1], w2_b[1])
+        def weigh(c):
             turned = psum.tile([P, PACK * CHUNK], F32, name=f"turned{c}", offset=(4 + c) * BANK)
             for t in range(PACK):
                 nc.tensor.transpose(
                     turned[:, t * CHUNK : (t + 1) * CHUNK], sig[c][:, t * P : (t + 1) * P], ident[:]
                 )
-            o = c * PACK * CHUNK
+            first = c * PACK * CHUNK
             nc.vector.tensor_tensor(
-                z_b[:, o : o + PACK * CHUNK].rearrange("p (c i t) -> p c t i", t=PACK, i=2),
-                turned[:].rearrange("p (t c i) -> p c t i", t=PACK, i=2),
+                z_b[:, first : first + PACK * CHUNK].rearrange("p (g i t) -> p g t i", t=PACK, i=2),
+                turned[:].rearrange("p (t g i) -> p g t i", t=PACK, i=2),
                 gn_b,
                 MULT,
             )
 
-        def product(m, bank, wq, ws, rq, rs, part=slice(0, S)):
+        quant(w2_q[0][:], w2_s[0][:], w2_b[0][:])
+        weave(nc.scalar.copy, w2_b[1][:, PACK * VECTOR_SHARE :], w2_raw[1][:, :, VECTOR_SHARE:])
+        weigh(0)
+        weigh(1)
+        quant(w2_q[1][:], w2_s[1][:], w2_b[1][:])
+        weigh(2)
+        weigh(3)
+
+        whole = slice(0, S)
+        halves = (slice(0, HALF), slice(HALF, S))
+        last = N // P - 1
+
+        def product(m, bank, w_q, w_s, moving_q, moving_s, part):
             cols = slice((m % 2) * P, (m % 2 + 1) * P)
             nc.tensor.matmul_mx(
                 out=bank[:, part],
-                lhsT=wq[m // 2][:, cols].bitcast(FP8X4),
-                lhsT_scale=ws[m // 2][:, cols],
-                rhs=rq[:, part].bitcast(FP8X4),
-                rhs_scale=rs[:, part],
+                lhsT=w_q[m // 2][:, cols].bitcast(FP8X4),
+                lhsT_scale=w_s[m // 2][:, cols],
+                rhs=moving_q[:, part].bitcast(FP8X4),
+                rhs_scale=moving_s[:, part],
                 start=True,
                 stop=True,
             )
 
-        halves = (slice(0, HALF), slice(HALF, S))
-
         def project(m):
-            bank = psum.tile([P, S], F32, name=f"valb{m}", offset=(2, 3, 0, 1)[m] * BANK)
-            product(m, bank, w2_q, w2_s, xo, xo_plane)
-            for part in halves if m == 3 else (slice(0, S),):
+            bank = psum.tile([P, S], F32, name=f"valb{m}", offset=VAL_BANKS[m] * BANK)
+            product(m, bank, w2_q, w2_s, xo, xo_plane, whole)
+            for part in halves if m == last else (whole,):
                 nc.scalar.copy(val[m][:, part], bank[:, part])
 
         def finish(m):
             if m == 0:
                 for a, part in enumerate(halves):
-                    bank = psum.tile([P, S], F32, name=f"h0_{a}", offset=(6, 4)[a] * BANK)
+                    bank = psum.tile([P, S], F32, name=f"h0_{a}", offset=H0_BANKS[a] * BANK)
                     product(m, bank, w1_q, w1_s, z_q, z_s, part)
                     nc.vector.tensor_tensor(res[m][:, part], bank[:, part], val[m][:, part], MULT)
             else:
-                bank = psum.tile([P, S], F32, name=f"h{m}", offset=(None, 5, 7, 2)[m] * BANK)
-                product(m, bank, w1_q, w1_s, z_q, z_s)
-                for part in halves if m == 3 else (slice(0, S),):
+                bank = psum.tile([P, S], F32, name=f"h{m}", offset=H_BANKS[m] * BANK)
+                product(m, bank, w1_q, w1_s, z_q, z_s, whole)
+                for part in halves if m == last else (whole,):
                     nc.vector.tensor_tensor(res[m][:, part], bank[:, part], val[m][:, part], MULT)
             nc.sync.dma_start(out[m * P : (m + 1) * P, :], res[m][:])
 
-        def quant_z(lo, hi):
-            cols = slice(lo * CHUNK, hi * CHUNK)
-            nc.vector.quantize_mx(
-                z_q[:, cols].bitcast(FP8X4),
-                z_s[:, cols],
-                z_b[:, lo * PACK * CHUNK : hi * PACK * CHUNK],
-            )
-
-        weave(nc.scalar.copy, w1_b[0], w1_raw[0])
-        weave(nc.scalar.copy, w1_b[1], w1_raw[1])
-        quant(w1_q[0], w1_s[0], w1_b[0])
-        quant_z(0, 2)
-        quant_z(2, 3)
-        quant_z(3, 4)
-        quant(w1_q[1], w1_s[1], w1_b[1])
-        for m in range(4):
+        for a in range(2):
+            weave(nc.scalar.copy, w1_b[a][:], w1_raw[a])
+        quant(w1_q[0][:], w1_s[0][:], w1_b[0][:])
+        for part in halves:
+            quant(z_q[:, part], z_s[:, part], z_b[:, PACK * part.start : PACK * part.stop])
+        quant(w1_q[1][:], w1_s[1][:], w1_b[1][:])
+        for m in range(N // P):
             project(m)
-        for m in range(4):
+        for m in range(N // P):
             finish(m)

@@ -26,7 +26,7 @@ RUN = 4
 BANK = 2048
 
 D_HEAD = G // 4
-VECTOR_SHARE = 64
+VECTOR_SHARE = 128
 
 ROW_BYTES = S * 4
 W2_AT = 0
@@ -241,7 +241,12 @@ def tile_picked_twostage_sigmoid_p_kernel(
 
         for a in range(2):
             weave(nc.scalar.copy, w1_b[a][:], w1_raw[a])
-        quant(w1_q[0][:], w1_s[0][:], w1_b[0][:])
+        for lo in (0, P):
+            quant(
+                w1_q[0][:, lo : lo + P],
+                w1_s[0][:, lo : lo + P],
+                w1_b[0][:, PACK * lo : PACK * (lo + P)],
+            )
         for part in halves:
             quant(z_q[:, part], z_s[:, part], z_b[:, PACK * part.start : PACK * part.stop])
         quant(w1_q[1][:], w1_s[1][:], w1_b[1][:])

@@ -25,7 +25,7 @@ W_HALF = N // 2
 RUN = 4
 BANK = 2048
 
-D_HEAD = G // 4
+D_HEAD = 3 * G // 16
 VECTOR_SHARE = 128
 
 ROW_BYTES = S * 4

@@ -26,7 +26,7 @@ RUN = 4
 BANK = 2048
 
 D_HEAD = 3 * G // 16
-VECTOR_SHARE = 128
+VECTOR_SHARE = 64
 
 ROW_BYTES = S * 4
 W2_AT = 0
@@ -150,23 +150,26 @@ def tile_picked_twostage_sigmoid_p_kernel(
 
         sig = []
         for c in range(S // CHUNK):
-            scores = psum.tile([P, H], F32, name=f"score{c}", offset=c * BANK)
-            nc.tensor.matmul_mx(
-                out=scores[:],
-                lhsT=xq[c].bitcast(FP8X4),
-                lhsT_scale=xq_plane[:, c * CHUNK : (c + 1) * CHUNK],
-                rhs=d_g[:].bitcast(FP8X4),
-                rhs_scale=d_plane,
-                start=True,
-                stop=True,
-            )
             sig.append(at(f"sig{c}", H, F32, SIG_AT + c * ROW_BYTES)[:])
-            nc.scalar.activation(
-                sig[c].rearrange("j (t g i) -> j g t i", t=PACK, i=RUN),
-                scores[:].rearrange("j (g i t) -> j g t i", t=PACK, i=RUN),
-                SIGMOID,
-                scale=0.0625,
-            )
+            for lo, hi in ((0, H // 2), (H // 2, H)) if c == 0 else ((0, H),):
+                bank = c if lo == 0 else 7
+                scores = psum.tile([P, H], F32, name=f"score{c}_{lo}", offset=bank * BANK)
+                nc.tensor.matmul_mx(
+                    out=scores[:, lo:hi],
+                    lhsT=xq[c].bitcast(FP8X4),
+                    lhsT_scale=xq_plane[:, c * CHUNK : (c + 1) * CHUNK],
+                    rhs=d_g[:, lo:hi].bitcast(FP8X4),
+                    rhs_scale=d_plane[:, lo:hi],
+                    start=True,
+                    stop=True,
+                )
+                groups = slice(lo // (PACK * RUN), hi // (PACK * RUN))
+                nc.scalar.activation(
+                    sig[c].rearrange("j (t g i) -> j g t i", t=PACK, i=RUN)[:, groups],
+                    scores[:, lo:hi].rearrange("j (g i t) -> j g t i", t=PACK, i=RUN),
+                    SIGMOID,
+                    scale=0.0625,
+                )
 
         gn_b = gn_t[:].unsqueeze(1).unsqueeze(3).to_broadcast([P, CHUNK // 2, PACK, 2])
         z_q = sb("z_q", S, U32)
@@ -206,6 +209,7 @@ def tile_picked_twostage_sigmoid_p_kernel(
 
         whole = slice(0, S)
         halves = (slice(0, HALF), slice(HALF, S))
+        tail = (slice(0, S - CHUNK), slice(S - CHUNK, S))
         last = N // P - 1
 
         def product(m, bank, w_q, w_s, moving_q, moving_s, part):
@@ -223,7 +227,7 @@ def tile_picked_twostage_sigmoid_p_kernel(
         def project(m):
             bank = psum.tile([P, S], F32, name=f"valb{m}", offset=VAL_BANKS[m] * BANK)
             product(m, bank, w2_q, w2_s, xo, xo_plane, whole)
-            for part in halves if m == last else (whole,):
+            for part in tail if m == last else (whole,):
                 nc.scalar.copy(val[m][:, part], bank[:, part])
 
         def finish(m):
@@ -235,7 +239,7 @@ def tile_picked_twostage_sigmoid_p_kernel(
             else:
                 bank = psum.tile([P, S], F32, name=f"h{m}", offset=H_BANKS[m] * BANK)
                 product(m, bank, w1_q, w1_s, z_q, z_s, whole)
-                for part in halves if m == last else (whole,):
+                for part in tail if m == last else (whole,):
                     nc.vector.tensor_tensor(res[m][:, part], bank[:, part], val[m][:, part], MULT)
             nc.sync.dma_start(out[m * P : (m + 1) * P, :], res[m][:])
 

@@ -37,7 +37,8 @@ VAL_AT = 10240
 SIG_AT = 20480
 LAST_SIG_AT = SIG_AT + 3 * ROW_BYTES
 
-VAL_BANKS = (2, 3, 0, 1)
+SCORE_BANKS = (0, 1, 2, 1)
+VAL_BANKS = (2, 1, 0, 3)
 H0_BANKS = (6, 4)
 H_BANKS = {1: 5, 2: 7, 3: 2}
 
@@ -152,7 +153,7 @@ def tile_picked_twostage_sigmoid_p_kernel(
         for c in range(S // CHUNK):
             sig.append(at(f"sig{c}", H, F32, SIG_AT + c * ROW_BYTES)[:])
             for lo, hi in ((0, H // 2), (H // 2, H)) if c == 0 else ((0, H),):
-                bank = c if lo == 0 else 7
+                bank = SCORE_BANKS[c] if lo == 0 else 7
                 scores = psum.tile([P, H], F32, name=f"score{c}_{lo}", offset=bank * BANK)
                 nc.tensor.matmul_mx(
                     out=scores[:, lo:hi],
@@ -202,8 +203,8 @@ def tile_picked_twostage_sigmoid_p_kernel(
         quant(w2_q[0][:], w2_s[0][:], w2_b[0][:])
         weave(nc.scalar.copy, w2_b[1][:, PACK * VECTOR_SHARE :], w2_raw[1][:, :, VECTOR_SHARE:])
         weigh(0)
-        weigh(1)
         quant(w2_q[1][:], w2_s[1][:], w2_b[1][:])
+        weigh(1)
         weigh(2)
         weigh(3)
 

@@ -25,7 +25,7 @@ W_HALF = N // 2
 RUN = 4
 BANK = 2048
 
-D_HEAD = 3 * G // 16
+D_HEAD = G // 8
 VECTOR_SHARE = 64
 
 ROW_BYTES = S * 4

from contextlib import ExitStack

import concourse.mybir as mybir
from concourse.masks import make_identity

K, T, S, N, G, H = 512, 2048, 512, 512, 2048, 512
FLOPS = 2 * K * H * S + 2 * H * N * S + 2 * K * N * S

F32 = mybir.dt.float32
BF16 = mybir.dt.bfloat16
I32 = mybir.dt.int32
U32 = mybir.dt.uint32
U16 = mybir.dt.uint16
U8 = mybir.dt.uint8
FP8X4 = mybir.dt.float8_e4m3fn_x4
SIGMOID = mybir.ActivationFunctionType.Sigmoid
MULT = mybir.AluOpType.mult

P = 128
PACK = 4
LIST_ROWS = 16
CHUNK = 128
HALF = S // 2
W_HALF = N // 2
RUN = 4
BANK = 2048

D_HEAD = G // 8
VECTOR_SHARE = 64

ROW_BYTES = S * 4
W2_AT = 0
D_SCALE_AT = 3072
W1_AT = (8192, 12288)
X_SCALE_AT = 11264
VAL_AT = 10240
SIG_AT = 20480
LAST_SIG_AT = SIG_AT + 3 * ROW_BYTES

SCORE_BANKS = (0, 1, 2, 1)
VAL_BANKS = (2, 1, 0, 3)
H0_BANKS = (6, 4)
H_BANKS = {1: 5, 2: 7, 3: 2}


def tile_picked_twostage_sigmoid_p_kernel(
    tc, x_words, x_scales, d_words, d_scales, gn, w1, w2, offs, kidx, own, out
):
    nc = tc.nc
    with ExitStack() as ctx:
        keep = ctx.enter_context(tc.tile_pool(name="keep", bufs=1))
        placed = ctx.enter_context(tc.tile_pool(name="placed", bufs=1))
        psum = ctx.enter_context(tc.psum_pool(name="psum", bufs=1))

        def sb(name, width, dtype):
            return keep.tile([P, width], dtype, name=name, tag=name, align_bytes=64)

        def at(name, width, dtype, offset):
            return placed.tile([P, width], dtype, name=name, align_bytes=64, offset=offset)

        kidx_t = keep.tile([P, H // LIST_ROWS], U16, name="kidx_t")
        offs_t = keep.tile([P, S // LIST_ROWS], U16, name="offs_t")
        own_t = keep.tile([P, S // LIST_ROWS], U16, name="own_t")

        d_scale_win = at("d_scale_win", G, U8, D_SCALE_AT)
        x_scale_win = at("x_scale_win", T, U8, X_SCALE_AT)
        score_planes = sb("score_planes", H + S, U8)
        xo_plane = sb("xo_plane", S, U8)
        ident = sb("ident", P, F32)
        nc.vector.memset(x_scale_win[:].bitcast(I32), 0)
        nc.vector.memset(d_scale_win[:].bitcast(I32), 0)
        nc.vector.memset(score_planes[:].bitcast(I32), 0)
        nc.vector.memset(xo_plane[:].bitcast(I32), 0)
        nc.vector.memset(ident[:], 0.0)
        make_identity(nc, ident[:], nomemset=True)

        d_win = sb("d_win", G, I32)
        x_win = sb("x_win", T, I32)
        gn_t = sb("gn_t", PACK, F32)

        d_rows = d_words[0].rearrange("p c r -> p (c r)").bitcast(I32)
        nc.sync.dma_start(d_win[:, 0:D_HEAD], d_rows[:, 0:D_HEAD])
        nc.sync.dma_start(offs_t[:], offs)
        nc.sync.dma_start(x_scale_win[0:P:8, :].bitcast(I32), x_scales[0].bitcast(I32))
        nc.sync.dma_start(kidx_t[:], kidx)
        nc.sync.dma_start(d_scale_win[0:P:8, :].bitcast(I32), d_scales[0].bitcast(I32))
        nc.sync.dma_start(d_win[:, D_HEAD:G], d_rows[:, D_HEAD:G])
        nc.sync.dma_start(own_t[:], own)
        nc.sync.dma_start(x_win[:], x_words[0].rearrange("p c r -> p (c r)").bitcast(I32))
        nc.sync.dma_start(gn_t[:], gn.rearrange("(p t) o -> p (t o)", t=PACK))

        def place(plane, spread):
            for r in range(4):
                nc.sync.dma_start(
                    plane[r:P:32, :].bitcast(I32),
                    spread[8 * r : P : 32, :].bitcast(I32),
                )

        score_g = sb("score_g", H + S, U8)
        nc.vector.tensor_copy(score_g[:, H:], x_scale_win[:].indirect(offs_t[:]))
        nc.vector.tensor_copy(score_g[:, :H], d_scale_win[:].indirect(kidx_t[:]))
        place(score_planes, score_g)
        d_plane = score_planes[:, :H]
        xq_plane = score_planes[:, H:]

        w2_whole = at("w2_whole", PACK * N, F32, W2_AT)
        nc.sync.dma_start(w2_whole[:], w2.rearrange("(p j) n -> p (j n)", j=PACK))
        w2_rows = w2_whole[:].rearrange("p (j n) -> p j n", j=PACK)
        w2_raw = [w2_rows[:, :, a * W_HALF : (a + 1) * W_HALF] for a in range(2)]
        w1_flat = [
            at("w1_raw0", PACK * W_HALF, F32, W1_AT[0])[:],
            at("w1_raw1", 3 * S, F32, W1_AT[1])[:, : PACK * W_HALF],
        ]
        w1_raw = [flat.rearrange("p (j n) -> p j n", j=PACK) for flat in w1_flat]

        d_g = sb("d_g", H, U32)
        nc.vector.tensor_copy(d_g[:], d_win[:].bitcast(U32).indirect(kidx_t[:]))
        xo_g = sb("xo_g", S, U8)
        nc.vector.tensor_copy(xo_g[:], x_scale_win[:].indirect(own_t[:]))
        place(xo_plane, xo_g)
        w1_rows = w1.rearrange("(p j) n -> p j n", j=PACK)
        for a in range(2):
            nc.sync.dma_start(w1_raw[a], w1_rows[:, :, a * W_HALF : (a + 1) * W_HALF])

        xq = []
        list_cols = CHUNK // LIST_ROWS
        for lo, hi in ((0, 1), (1, 2), (2, 4)):
            piece = sb(f"xq{lo}", (hi - lo) * CHUNK, U32)
            nc.vector.tensor_copy(
                piece[:], x_win[:].bitcast(U32).indirect(offs_t[:, lo * list_cols : hi * list_cols])
            )
            xq.extend(piece[:, i * CHUNK : (i + 1) * CHUNK] for i in range(hi - lo))
        xo = sb("xo", S, U32)
        nc.vector.tensor_copy(xo[:], x_win[:].bitcast(U32).indirect(own_t[:]))

        w2_b = [sb(f"w2_b{a}", PACK * W_HALF, BF16) for a in range(2)]
        w1_b = [sb(f"w1_b{a}", PACK * W_HALF, BF16) for a in range(2)]

        def weave(copy, dst, rows):
            copy(
                dst.rearrange("p (c i j) -> p c j i", i=RUN, j=PACK),
                rows.rearrange("p j (c i) -> p c j i", i=RUN),
            )

        weave(nc.vector.tensor_copy, w2_b[0][:], w2_raw[0])
        weave(
            nc.vector.tensor_copy,
            w2_b[1][:, : PACK * VECTOR_SHARE],
            w2_raw[1][:, :, :VECTOR_SHARE],
        )

        sig = []
        for c in range(S // CHUNK):
            sig.append(at(f"sig{c}", H, F32, SIG_AT + c * ROW_BYTES)[:])
            for lo, hi in ((0, H // 2), (H // 2, H)) if c == 0 else ((0, H),):
                bank = SCORE_BANKS[c] if lo == 0 else 7
                scores = psum.tile([P, H], F32, name=f"score{c}_{lo}", offset=bank * BANK)
                nc.tensor.matmul_mx(
                    out=scores[:, lo:hi],
                    lhsT=xq[c].bitcast(FP8X4),
                    lhsT_scale=xq_plane[:, c * CHUNK : (c + 1) * CHUNK],
                    rhs=d_g[:, lo:hi].bitcast(FP8X4),
                    rhs_scale=d_plane[:, lo:hi],
                    start=True,
                    stop=True,
                )
                groups = slice(lo // (PACK * RUN), hi // (PACK * RUN))
                nc.scalar.activation(
                    sig[c].rearrange("j (t g i) -> j g t i", t=PACK, i=RUN)[:, groups],
                    scores[:, lo:hi].rearrange("j (g i t) -> j g t i", t=PACK, i=RUN),
                    SIGMOID,
                    scale=0.0625,
                )

        gn_b = gn_t[:].unsqueeze(1).unsqueeze(3).to_broadcast([P, CHUNK // 2, PACK, 2])
        z_q = sb("z_q", S, U32)
        z_s = at("z_s", S, U8, LAST_SIG_AT + 4 * W_HALF)
        z_b = sb("z_b", PACK * S, BF16)
        w2_q = [sb(f"w2_q{a}", W_HALF, U32) for a in range(2)]
        w2_s = [sb(f"w2_s{a}", W_HALF, U8) for a in range(2)]
        w1_q = [sb(f"w1_q{a}", W_HALF, U32) for a in range(2)]
        w1_s = [at(f"w1_s{a}", W_HALF, U8, LAST_SIG_AT + W_HALF * (a + 1)) for a in range(2)]
        val = [at(f"val{m}", S, F32, VAL_AT + m * ROW_BYTES) for m in range(N // P)]
        res = [sb(f"res{m}", S, F32) for m in range(N // P)]

        def quant(codes, plane, woven):
            nc.vector.quantize_mx(codes.bitcast(FP8X4), plane, woven)

        def weigh(c):
            turned = psum.tile([P, PACK * CHUNK], F32, name=f"turned{c}", offset=(4 + c) * BANK)
            for t in range(PACK):
                nc.tensor.transpose(
                    turned[:, t * CHUNK : (t + 1) * CHUNK], sig[c][:, t * P : (t + 1) * P], ident[:]
                )
            first = c * PACK * CHUNK
            nc.vector.tensor_tensor(
                z_b[:, first : first + PACK * CHUNK].rearrange("p (g i t) -> p g t i", t=PACK, i=2),
                turned[:].rearrange("p (t g i) -> p g t i", t=PACK, i=2),
                gn_b,
                MULT,
            )

        quant(w2_q[0][:], w2_s[0][:], w2_b[0][:])
        weave(nc.scalar.copy, w2_b[1][:, PACK * VECTOR_SHARE :], w2_raw[1][:, :, VECTOR_SHARE:])
        weigh(0)
        quant(w2_q[1][:], w2_s[1][:], w2_b[1][:])
        weigh(1)
        weigh(2)
        weigh(3)

        whole = slice(0, S)
        halves = (slice(0, HALF), slice(HALF, S))
        tail = (slice(0, S - CHUNK), slice(S - CHUNK, S))
        last = N // P - 1

        def product(m, bank, w_q, w_s, moving_q, moving_s, part):
            cols = slice((m % 2) * P, (m % 2 + 1) * P)
            nc.tensor.matmul_mx(
                out=bank[:, part],
                lhsT=w_q[m // 2][:, cols].bitcast(FP8X4),
                lhsT_scale=w_s[m // 2][:, cols],
                rhs=moving_q[:, part].bitcast(FP8X4),
                rhs_scale=moving_s[:, part],
                start=True,
                stop=True,
            )

        def project(m):
            bank = psum.tile([P, S], F32, name=f"valb{m}", offset=VAL_BANKS[m] * BANK)
            product(m, bank, w2_q, w2_s, xo, xo_plane, whole)
            for part in tail if m == last else (whole,):
                nc.scalar.copy(val[m][:, part], bank[:, part])

        def finish(m):
            if m == 0:
                for a, part in enumerate(halves):
                    bank = psum.tile([P, S], F32, name=f"h0_{a}", offset=H0_BANKS[a] * BANK)
                    product(m, bank, w1_q, w1_s, z_q, z_s, part)
                    nc.vector.tensor_tensor(res[m][:, part], bank[:, part], val[m][:, part], MULT)
            else:
                bank = psum.tile([P, S], F32, name=f"h{m}", offset=H_BANKS[m] * BANK)
                product(m, bank, w1_q, w1_s, z_q, z_s, whole)
                for part in tail if m == last else (whole,):
                    nc.vector.tensor_tensor(res[m][:, part], bank[:, part], val[m][:, part], MULT)
            nc.sync.dma_start(out[m * P : (m + 1) * P, :], res[m][:])

        for a in range(2):
            weave(nc.scalar.copy, w1_b[a][:], w1_raw[a])
        for lo in (0, P):
            quant(
                w1_q[0][:, lo : lo + P],
                w1_s[0][:, lo : lo + P],
                w1_b[0][:, PACK * lo : PACK * (lo + P)],
            )
        for part in halves:
            quant(z_q[:, part], z_s[:, part], z_b[:, PACK * part.start : PACK * part.stop])
        quant(w1_q[1][:], w1_s[1][:], w1_b[1][:])
        for m in range(N // P):
            project(m)
        for m in range(N // P):
            finish(m)
